import numpy as np
import ml_dtypes


def mxq(x, axis, fmt="e4m3"):
    dtype, down = {"e4m3": (ml_dtypes.float8_e4m3fn, 7), "e5m2": (ml_dtypes.float8_e5m2, 14)}[fmt]
    v = np.moveaxis(np.asarray(x, np.float32).astype(ml_dtypes.bfloat16).astype(np.float64), axis, -1)
    blocks = v.reshape(v.shape[:-1] + (-1, 32))
    amax = np.abs(blocks).max(-1, keepdims=True)
    byte = np.maximum(np.where(amax > 0, np.frexp(amax)[1] - 1 + 127, 0) - down, 1)
    scale = np.exp2(byte - 127.0)
    codes = (blocks / scale).astype(np.float32).astype(dtype).astype(np.float64)
    return np.moveaxis((codes * scale).reshape(v.shape), -1, axis)


WIDE = False


def mx_kscale(k):
    if not WIDE:
        return np.ones(k)
    levels = np.array([10, -10, 5, -5, 0])
    if k % 512:
        return np.exp2(np.random.permutation(np.resize(levels, k // 32))).repeat(32)
    a = np.empty((k // 512, 16))
    for p in range(k // 512):
        a[p, :8] = np.random.permutation(np.resize(levels, 8))
        for g in range(8):
            far = levels[np.abs(levels - a[p, g]) >= 10]
            a[p, g + 8] = far[np.random.randint(len(far))]
    return np.exp2(a.ravel()).repeat(32)


def f64(x):
    return np.asarray(x).astype(np.float64)


def striped(idx):
    return np.tile(idx.reshape(-1, 16).T, (8, 1)).astype(np.uint16)


def unstriped(offs):
    return offs[:16].T.reshape(-1).astype(np.int64)


E2M1 = np.array([0.0, 0.5, 1.0, 1.5, 2.0, 3.0, 4.0, 6.0, -0.0, -0.5, -1.0, -1.5, -2.0, -3.0, -4.0, -6.0])


def pack_weight(w, fmt):
    k, n = w.shape
    w = f64(np.asarray(w, np.float32).astype(ml_dtypes.bfloat16)).reshape(k // 32, 32, n)
    amax = np.abs(w).max(1)
    if fmt == "e4m3":
        byte = np.frexp(amax)[1] - 1 + 127 - 7
    else:
        mant, ex = np.frexp(amax / 6.0)
        byte = np.where(mant > 0.5, ex, ex - 1) + 127
    byte = np.clip(np.where(amax > 0, byte, 1), 1, 254)
    scaled = (w * np.exp2(127.0 - byte)[:, None, :]).reshape(k, n).astype(np.float32)
    by_word = np.ascontiguousarray(scaled.reshape(k // 512, 128, 4, n).transpose(0, 1, 3, 2))
    if fmt == "e4m3":
        words = by_word.astype(ml_dtypes.float8_e4m3fn).view(np.uint8)
    else:
        c = by_word.astype(ml_dtypes.float4_e2m1fn).view(np.uint8) & 0xF
        words = (c[..., 0::2] | (c[..., 1::2] << 4)).reshape(k // 512, 128, 2 * n)
    return np.ascontiguousarray(words), np.ascontiguousarray(byte.astype(np.uint8).reshape(k // 512, 16, n))


def unpack_weight(words, scales, fmt):
    g, _, n = scales.shape
    words = np.ascontiguousarray(words).reshape(g, 128, n, -1)
    if fmt == "e4m3":
        vals = words.view(ml_dtypes.float8_e4m3fn).astype(np.float64)
    else:
        nib = np.empty((g, 128, n, 4), np.uint8)
        nib[..., 0::2] = words & 0xF
        nib[..., 1::2] = words >> 4
        vals = E2M1[nib]
    vals = vals * np.repeat(np.exp2(scales.astype(np.float64) - 127.0), 8, axis=1)[..., None]
    return vals.transpose(0, 1, 3, 2).reshape(g * 512, n)


def planes(y):
    n, m = y.shape
    v = y.astype(np.float32).astype(ml_dtypes.bfloat16).astype(np.float64).reshape(n // 32, 32, m)
    top = np.abs(v).max(1)
    byte = np.clip(np.where(top > 0, np.frexp(top)[1] - 1 + 127 - 7, 1), 1, 254)
    codes = (v * np.exp2(127.0 - byte)[:, None, :]).reshape(n, m).astype(np.float32).astype(ml_dtypes.float8_e4m3fn).view(np.uint8)
    words = codes.reshape(n // 512, 128, 4, m).transpose(0, 1, 3, 2)
    return np.ascontiguousarray(words), np.ascontiguousarray(byte.astype(np.uint8).reshape(n // 512, 16, m))


def silu(v):
    return v / (1.0 + np.exp(-np.maximum(v, -700.0)))


K, T, E, C, H, N, HOT = 512, 768, 9, 256, 512, 512, 4
TOP = 3


def by_expert(wq, xq):
    return np.concatenate([wq[e].T @ xq[:, e * C:(e + 1) * C] for e in range(E)], axis=1)


def setup_inputs():
    n = np.random.standard_normal
    s = mx_kscale(K)
    u = mx_kscale(H)
    deal = np.repeat(np.arange(E), C).reshape(TOP, T)[:, np.random.permutation(T)]
    deal = np.take_along_axis(deal, np.argsort(np.random.rand(TOP, T), axis=0), axis=0)
    for _ in range(8):
        s_, t_ = np.random.permutation(T).reshape(2, -1); r = np.random.randint(TOP, size=T // 2); x, y = deal[r, s_].copy(), deal[r, t_].copy()
        ok = ~((deal[:, s_] == y).any(0) | (deal[:, t_] == x).any(0)); deal[r[ok], s_[ok]] = y[ok]; deal[r[ok], t_[ok]] = x[ok]
    order = np.lexsort((np.random.rand(TOP * T), deal.reshape(-1)))
    slot_token = order % T; pos = np.empty(TOP * T, np.int64); pos[order] = np.arange(TOP * T); pos = pos.reshape(TOP, T)
    g = np.random.uniform(0.5, 1.5, (TOP, T)); g = g / g.sum(0)
    x = pack_weight(n((K, T)) * s[:, None], "e4m3")
    w1h = [pack_weight(m, "e4m3") for m in n((HOT, K, H)) / np.sqrt(K) / s[None, :, None] * u]
    w2h = [pack_weight(m, "e4m3") for m in n((HOT, H, N)) / np.sqrt(H) / u[None, :, None]]
    w1c = [pack_weight(m, "e2m1") for m in n((E - HOT, K, H)) / np.sqrt(K) / s[None, :, None] * u]
    w2c = [pack_weight(m, "e2m1") for m in n((E - HOT, H, N)) / np.sqrt(H) / u[None, :, None]]
    return {
        "x_words": x[0],
        "x_scales": x[1],
        "w1h_words": np.stack([m[0] for m in w1h]),
        "w1h_scales": np.stack([m[1] for m in w1h]),
        "w2h_words": np.stack([m[0] for m in w2h]),
        "w2h_scales": np.stack([m[1] for m in w2h]),
        "w1c_words": np.stack([m[0] for m in w1c]),
        "w1c_scales": np.stack([m[1] for m in w1c]),
        "w2c_words": np.stack([m[0] for m in w2c]),
        "w2c_scales": np.stack([m[1] for m in w2c]),
        "gate": np.stack([np.tile(r, (128, 1)) for r in g]).astype(np.float32),
        "offs": striped(slot_token),
        "pos1": striped(pos[0]),
        "pos2": striped(pos[1]),
        "pos3": striped(pos[2]),
    }


def reference(x_words, x_scales, w1h_words, w1h_scales, w2h_words, w2h_scales, w1c_words, w1c_scales, w2c_words, w2c_scales, gate, offs, pos1, pos2, pos3):
    w1h = np.stack([unpack_weight(w1h_words[e], w1h_scales[e], "e4m3") for e in range(HOT)])
    w2h = np.stack([unpack_weight(w2h_words[e], w2h_scales[e], "e4m3") for e in range(HOT)])
    w1c = np.stack([unpack_weight(w1c_words[e], w1c_scales[e], "e2m1") for e in range(E - HOT)])
    w2c = np.stack([unpack_weight(w2c_words[e], w2c_scales[e], "e2m1") for e in range(E - HOT)])
    idx = unstriped(offs)
    xq = unpack_weight(x_words, x_scales, "e4m3")[:, idx]
    w1 = [*w1h, *w1c]
    w2 = [*w2h, *w2c]
    h = silu(by_expert(w1, xq))
    y = by_expert(w2, mxq(h, 0, "e4m3"))
    out = sum(f64(gate[r, :1]) * y[:, unstriped(p)] for r, p in enumerate((pos1, pos2, pos3)))
    out_0 = out
    return (out_0,) + planes(out_0)

@@ -1,0 +1,231 @@
+from contextlib import ExitStack
+
+import concourse.mybir as mybir
+from concourse.masks import make_identity
+
+K, T, E, C, H, N, HOT = 512, 768, 9, 256, 512, 512, 4
+COLD = E - HOT
+TOP = 3
+S = E * C
+P = 128
+FLOPS = 2 * S * (K * H + H * N)
+
+F32 = mybir.dt.float32
+BF16 = mybir.dt.bfloat16
+I32 = mybir.dt.int32
+U32 = mybir.dt.uint32
+U16 = mybir.dt.uint16
+U8 = mybir.dt.uint8
+FP8X4 = mybir.dt.float8_e4m3fn_x4
+FP4X4 = mybir.dt.float4_e2m1fn_x4
+SILU = mybir.ActivationFunctionType.Silu
+MULT = mybir.AluOpType.mult
+
+SLOT_PIECES = [128, 128] + [256] * 8
+TOKEN_GROUPS = [(0, 1), (2, 3), (4,), (5,)]
+WORDS_ON_SCALAR = (5, 6, 7, 8)
+Y_ON_VECTOR = (3,)
+
+
+def tile_moe_hot_mlp_silu_kernel(
+    tc, x_words, x_scales, w1h_words, w1h_scales, w2h_words, w2h_scales, w1c_words, w1c_scales,
+    w2c_words, w2c_scales, gate, offs, pos1, pos2, pos3, out_0, out_1, out_2,
+):
+    nc = tc.nc
+    with ExitStack() as ctx:
+        keep = ctx.enter_context(tc.tile_pool(name="keep", bufs=1))
+        psum = ctx.enter_context(tc.psum_pool(name="psum", bufs=1))
+
+        def sb(name, shape, dtype, tag=None):
+            return keep.tile(shape, dtype, name=name, tag=tag or name, align_bytes=64)
+
+        banks = [psum.tile([P, 512], F32, name="bank%d" % b) for b in range(8)]
+
+        offs_sb = sb("offs_sb", [P, S // 16], U16)
+        pos_sb = [sb("pos_sb%d" % r, [P, T // 16], U16) for r in range(TOP)]
+        xw = sb("xw", [P, T], I32)
+        xs = sb("xs", [P, T], U8)
+        w1h_first = sb("w1h_first", [P, H], I32)
+        s1h = sb("s1h", [P, H], U8)
+        s2h = sb("s2h", [P, N], U8)
+        s1c = sb("s1c", [P, COLD, H], U8)
+        s2c = sb("s2c", [P, COLD, N], U8)
+        ident = sb("ident", [P, P], F32)
+        warm_in = sb("warm_in", [P, 1], F32)
+        warm_out = sb("warm_out", [P, 1], F32)
+
+        nc.vector.memset(s1h[:].bitcast(I32), 0)
+        nc.vector.memset(warm_in[:], 0.0)
+        nc.scalar.activation(warm_out[:], warm_in[:], SILU)
+        nc.vector.memset(s1c[:].bitcast(I32), 0)
+        nc.vector.memset(s2h[:].bitcast(I32), 0)
+        nc.vector.memset(s2c[:].bitcast(I32), 0)
+        make_identity(nc, ident[:])
+
+        def load_hot_scales(dst, src):
+            for q in range(4):
+                nc.sync.dma_start(dst[32 * q : 32 * q + 16, :].bitcast(I32), src[:, 0, 4 * q : 4 * q + 4, :].bitcast(I32))
+
+        def load_cold_scales(dst, src):
+            for r in range(4):
+                nc.sync.dma_start(dst[r:P:32].bitcast(I32), src[:, 0, r:16:4, :].rearrange("e q c -> q e c").bitcast(I32))
+
+        def hot_words(src, lo, hi):
+            return src[lo:hi, 0].rearrange("e p c d -> p e (c d)").bitcast(I32)
+
+        nc.sync.dma_start(xw[:], x_words[0].rearrange("p t d -> p (t d)").bitcast(I32))
+        for r in range(4):
+            nc.sync.dma_start(xs[32 * r : 32 * r + 32, :].bitcast(I32),
+                              x_scales[0, 4 * r : 4 * r + 4, :].bitcast(I32).unsqueeze(0).to_broadcast([8, 4, T // 4]))
+        nc.sync.dma_start(offs_sb[:], offs)
+        nc.sync.dma_start(w1h_first[:], w1h_words[0, 0].rearrange("p c d -> p (c d)").bitcast(I32))
+        load_hot_scales(s1h, w1h_scales)
+        w1h_rest = sb("w1h_rest", [P, HOT - 1, H], I32, tag="warm_in")
+        w1c = sb("w1c", [P, COLD, 2 * H], U8, tag="warm_out")
+        nc.sync.dma_start(w1h_rest[:], hot_words(w1h_words, 1, HOT))
+        load_cold_scales(s1c, w1c_scales)
+        nc.sync.dma_start(w1c[:].bitcast(I32), w1c_words[:, 0].rearrange("e p b -> p e b").bitcast(I32))
+        load_hot_scales(s2h, w2h_scales)
+        load_cold_scales(s2c, w2c_scales)
+        for r, pos in enumerate((pos1, pos2, pos3)):
+            nc.sync.dma_start(pos_sb[r][:], pos)
+
+        chunk_words, chunk_scales = [], []
+        slot0 = 0
+        for j, n in enumerate(SLOT_PIECES):
+            piece = offs_sb[:, slot0 // 16 : (slot0 + n) // 16]
+            gw = sb("gw%d" % j, [P, n], U32)
+            gs = sb("gs%d" % j, [P, n], U8)
+            nc.vector.tensor_copy(gw[:], xw[:].bitcast(U32).indirect(piece))
+            nc.vector.tensor_copy(gs[:], xs[:].indirect(piece))
+            for c in range(n // P):
+                chunk_words.append(gw[:, c * P : (c + 1) * P])
+                chunk_scales.append(gs[:, c * P : (c + 1) * P])
+            slot0 = slot0 + n
+
+        gate_sb = sb("gate_sb", [P, TOP, T], F32, tag="xw")
+        nc.sync.dma_start(gate_sb[:], gate.rearrange("r p t -> p r t"))
+
+        h_rows = []
+        for k in range(S // P):
+            e = k * P // C
+            if e == 0:
+                w, ws = w1h_first[:].bitcast(FP8X4), s1h[:, :]
+            elif e < HOT:
+                w, ws = w1h_rest[:, e - 1, :].bitcast(FP8X4), s1h[4 * e : P, :]
+            else:
+                w, ws = w1c[:, e - HOT, :].bitcast(FP4X4), s1c[:, e - HOT, :]
+            bank = banks[k % 7]
+            nc.tensor.matmul_mx(bank[:], lhsT=chunk_words[k].bitcast(FP8X4), lhsT_scale=chunk_scales[k],
+                                rhs=w, rhs_scale=ws, start=True, stop=True)
+            rows = sb("h_rows%d" % k, [P, H], BF16)
+            nc.scalar.activation(rows[:].rearrange("s (u p e) -> s u p e", u=2, e=2),
+                                 bank[:].rearrange("s (p u e) -> s u p e", u=2, e=2), SILU)
+            h_rows.append(rows)
+
+        w2 = sb("w2", [P, HOT * 4 * N + COLD * 2 * N], U8, tag="w1h_first")
+        w2h = w2[:, 0 : HOT * 4 * N].bitcast(I32).rearrange("p (e c) -> p e c", e=HOT)
+        w2c = w2[:, HOT * 4 * N :].rearrange("p (e c) -> p e c", e=COLD)
+        nc.sync.dma_start(w2h, hot_words(w2h_words, 0, HOT))
+        nc.sync.dma_start(w2c.bitcast(I32), w2c_words[:, 0].rearrange("e p b -> p e b").bitcast(I32))
+
+        turn_bank = [7, 4, 5, 6, 0, 1, 2, 3, 7]
+        h_in = [sb("h_in%d" % e, [P, 4 * C], BF16) for e in range(E)]
+        h_codes = [sb("h_codes%d" % e, [P, C], U32) for e in range(E)]
+        h_scales = [sb("h_scales%d" % e, [P, C], U8) for e in range(E)]
+
+        def turn(e):
+            bank = banks[turn_bank[e]]
+            for c in range(2):
+                words = h_rows[2 * e + c][:].bitcast(F32)
+                for u in range(2):
+                    col = (2 * c + u) * P
+                    nc.tensor.transpose(bank[:, col : col + P], words[:, u * P : (u + 1) * P], ident[:])
+            dst = h_in[e][:].bitcast(F32).rearrange("p (c s u) -> p c s u", c=2, u=2)
+            src = bank[:].rearrange("p (c u s) -> p c s u", c=2, u=2)
+            if e in WORDS_ON_SCALAR:
+                nc.scalar.copy(dst, src)
+            else:
+                nc.vector.tensor_copy(dst, src)
+
+        def quantise(e):
+            nc.vector.quantize_mx(h_codes[e][:].bitcast(FP8X4), h_scales[e][:], h_in[e][:])
+
+        turn(0)
+        for e in range(1, E):
+            turn(e)
+            quantise(e - 1)
+        quantise(E - 1)
+
+        y = [sb("y%d" % b, [P, S], F32) for b in range(4)]
+        second_bank = [4, 5, 6, 0, 1, 2, 3, 7]
+        for u in range(20):
+            b, pair = divmod(u, 5)
+            bank = banks[second_bank[u % 8]]
+            experts = range(2 * pair, min(2 * pair + 2, E))
+            for e in experts:
+                if e < HOT:
+                    w, ws = w2h[:, e, b * P : (b + 1) * P].bitcast(FP8X4), s2h[4 * e : P, b * P : (b + 1) * P]
+                else:
+                    w, ws = w2c[:, e - HOT, 2 * b * P : 2 * (b + 1) * P].bitcast(FP4X4), s2c[:, e - HOT, b * P : (b + 1) * P]
+                nc.tensor.matmul_mx(bank[:, (e % 2) * C : (e % 2 + 1) * C], lhsT=w, lhsT_scale=ws,
+                                    rhs=h_codes[e][:].bitcast(FP8X4), rhs_scale=h_scales[e][:], start=True, stop=True)
+            width = len(experts) * C
+            dst = y[b][:, 2 * pair * C : 2 * pair * C + width]
+            if u in Y_ON_VECTOR:
+                nc.vector.tensor_copy(dst, bank[:, 0:width])
+            else:
+                nc.scalar.copy(dst, bank[:, 0:width])
+
+        sum_bank = [1, 2, 3, 7, 6, 0]
+        back_bank = [4, 5]
+        first = [sb("first%d" % r, [P, T], F32) for r in range(TOP)]
+        ring = [[sb("ring%d_%d" % (j, r), [P, 2 * P], F32) for r in range(TOP)] for j in range(3)]
+        out_codes = sb("out_codes", [P, T], I32)
+        out_scales = sb("out_scales", [P, T], U8)
+        out_rows = out_0.rearrange("(p t) k -> p t k", t=4)
+        out_words = out_1[0].rearrange("p t d -> p (t d)").bitcast(I32)
+
+        def weigh(dst, b, r, t0, n):
+            nc.vector.tensor_tensor(dst, y[b][:].indirect(pos_sb[r][:, t0 // 16 : (t0 + n) // 16]),
+                                    gate_sb[:, r, t0 : t0 + n], MULT)
+
+        def add_up(c, b, r, src):
+            nc.tensor.matmul(banks[sum_bank[c]][:, b * P : (b + 1) * P], lhsT=src, rhs=ident[:],
+                             is_transpose=True, start=(r == 0), stop=(r == TOP - 1))
+
+        for r in range(TOP):
+            weigh(first[r][:], 0, r, 0, T)
+        for c in range(T // P):
+            for r in range(TOP):
+                add_up(c, 0, r, first[r][:, c * P : (c + 1) * P])
+
+        for g, chunks in enumerate(TOKEN_GROUPS):
+            t0, n = chunks[0] * P, len(chunks) * P
+            for b in range(1, 4):
+                slot = ring[(b - 1 - g) % 3]
+                for r in range(TOP):
+                    weigh(slot[r][:, 0:n], b, r, t0, n)
+                    for j, c in enumerate(chunks):
+                        add_up(c, b, r, slot[r][:, j * P : (j + 1) * P])
+            result = sb("result%d" % g, [P, 4, n], F32)
+            rounded = sb("rounded%d" % g, [P, n, 4], BF16)
+            for j, c in enumerate(chunks):
+                sums = sb("sums%d" % c, [P, 4, P], F32)
+                nc.scalar.copy(sums[:], banks[sum_bank[c]][:].rearrange("k (p t) -> k t p", t=4))
+                bank = banks[back_bank[c % 2]]
+                for t in range(4):
+                    nc.tensor.transpose(bank[:, t * P : (t + 1) * P], sums[:, t, :], ident[:])
+                view = bank[:].rearrange("p (t k) -> p t k", t=4)
+                if len(chunks) == 2:
+                    nc.scalar.copy(result[:, :, j * P : (j + 1) * P], view)
+                    nc.scalar.copy(rounded[:, j * P : (j + 1) * P, :], view.rearrange("p t k -> p k t"))
+                else:
+                    nc.vector.tensor_copy(rounded[:, j * P : (j + 1) * P, :], view.rearrange("p t k -> p k t"))
+                    nc.scalar.copy(result[:, :, j * P : (j + 1) * P], view)
+            nc.sync.dma_start(out_rows[:, :, t0 : t0 + n], result[:])
+            nc.vector.quantize_mx(out_codes[:, t0 : t0 + n].bitcast(FP8X4), out_scales[:, t0 : t0 + n],
+                                  rounded[:].rearrange("p k t -> p (k t)"))
+            nc.sync.dma_start(out_words[:, t0 : t0 + n], out_codes[:, t0 : t0 + n])
+        for r in range(4):
+            nc.sync.dma_start(out_2[0, r:16:4, :].bitcast(I32), out_scales[r:P:32, :].bitcast(I32))

@@ -21,10 +21,10 @@ FP4X4 = mybir.dt.float4_e2m1fn_x4
 SILU = mybir.ActivationFunctionType.Silu
 MULT = mybir.AluOpType.mult
 
-SLOT_PIECES = [128, 128] + [256] * 8
+SLOT_PIECES = [128, 128] + [256] * 7 + [128, 128]
 TOKEN_GROUPS = [(0, 1), (2, 3), (4,), (5,)]
-WORDS_ON_SCALAR = (5, 6, 7, 8)
-Y_ON_VECTOR = (3,)
+WORDS_ON_SCALAR = (3, 4, 5, 6, 7, 8)
+Y_ON_VECTOR = (2, 3)
 
 
 def tile_moe_hot_mlp_silu_kernel(
@@ -73,10 +73,10 @@ def tile_moe_hot_mlp_silu_kernel(
         def hot_words(src, lo, hi):
             return src[lo:hi, 0].rearrange("e p c d -> p e (c d)").bitcast(I32)
 
-        nc.sync.dma_start(xw[:], x_words[0].rearrange("p t d -> p (t d)").bitcast(I32))
         for r in range(4):
             nc.sync.dma_start(xs[32 * r : 32 * r + 32, :].bitcast(I32),
                               x_scales[0, 4 * r : 4 * r + 4, :].bitcast(I32).unsqueeze(0).to_broadcast([8, 4, T // 4]))
+        nc.sync.dma_start(xw[:], x_words[0].rearrange("p t d -> p (t d)").bitcast(I32))
         nc.sync.dma_start(offs_sb[:], offs)
         nc.sync.dma_start(w1h_first[:], w1h_words[0, 0].rearrange("p c d -> p (c d)").bitcast(I32))
         load_hot_scales(s1h, w1h_scales)
@@ -103,9 +103,6 @@ def tile_moe_hot_mlp_silu_kernel(
                 chunk_scales.append(gs[:, c * P : (c + 1) * P])
             slot0 = slot0 + n
 
-        gate_sb = sb("gate_sb", [P, TOP, T], F32, tag="xw")
-        nc.sync.dma_start(gate_sb[:], gate.rearrange("r p t -> p r t"))
-
         h_rows = []
         for k in range(S // P):
             e = k * P // C
@@ -129,10 +126,14 @@ def tile_moe_hot_mlp_silu_kernel(
         nc.sync.dma_start(w2h, hot_words(w2h_words, 0, HOT))
         nc.sync.dma_start(w2c.bitcast(I32), w2c_words[:, 0].rearrange("e p b -> p e b").bitcast(I32))
 
+        gate_sb = sb("gate_sb", [P, TOP, T], F32, tag="warm_in")
+        nc.sync.dma_start(gate_sb[:], gate.rearrange("r p t -> p r t"))
+
         turn_bank = [7, 4, 5, 6, 0, 1, 2, 3, 7]
-        h_in = [sb("h_in%d" % e, [P, 4 * C], BF16) for e in range(E)]
-        h_codes = [sb("h_codes%d" % e, [P, C], U32) for e in range(E)]
-        h_scales = [sb("h_scales%d" % e, [P, C], U8) for e in range(E)]
+        pair_width = [min(2 * C, S - 2 * C * j) for j in range(5)]
+        h_in = [sb("h_in%d" % j, [P, 4 * n], BF16) for j, n in enumerate(pair_width)]
+        h_codes = [sb("h_codes%d" % j, [P, n], U32) for j, n in enumerate(pair_width)]
+        h_scales = [sb("h_scales%d" % j, [P, n], U8) for j, n in enumerate(pair_width)]
 
         def turn(e):
             bank = banks[turn_bank[e]]
@@ -141,7 +142,7 @@ def tile_moe_hot_mlp_silu_kernel(
                 for u in range(2):
                     col = (2 * c + u) * P
                     nc.tensor.transpose(bank[:, col : col + P], words[:, u * P : (u + 1) * P], ident[:])
-            dst = h_in[e][:].bitcast(F32).rearrange("p (c s u) -> p c s u", c=2, u=2)
+            dst = h_in[e // 2][:, (e % 2) * 4 * C : (e % 2 + 1) * 4 * C].bitcast(F32).rearrange("p (c s u) -> p c s u", c=2, u=2)
             src = bank[:].rearrange("p (c u s) -> p c s u", c=2, u=2)
             if e in WORDS_ON_SCALAR:
                 nc.scalar.copy(dst, src)
@@ -151,14 +152,14 @@ def tile_moe_hot_mlp_silu_kernel(
         def quantise(e):
             nc.vector.quantize_mx(h_codes[e][:].bitcast(FP8X4), h_scales[e][:], h_in[e][:])
 
-        turn(0)
-        for e in range(1, E):
+        for e in range(E):
             turn(e)
-            quantise(e - 1)
-        quantise(E - 1)
+            if e >= 2 and e % 2 == 0:
+                quantise(e // 2 - 1)
+        quantise(E // 2)
 
         y = [sb("y%d" % b, [P, S], F32) for b in range(4)]
-        second_bank = [4, 5, 6, 0, 1, 2, 3, 7]
+        second_bank = [6, 0, 1, 4, 5, 2, 3, 7]
         for u in range(20):
             b, pair = divmod(u, 5)
             bank = banks[second_bank[u % 8]]
@@ -168,8 +169,9 @@ def tile_moe_hot_mlp_silu_kernel(
                     w, ws = w2h[:, e, b * P : (b + 1) * P].bitcast(FP8X4), s2h[4 * e : P, b * P : (b + 1) * P]
                 else:
                     w, ws = w2c[:, e - HOT, 2 * b * P : 2 * (b + 1) * P].bitcast(FP4X4), s2c[:, e - HOT, b * P : (b + 1) * P]
-                nc.tensor.matmul_mx(bank[:, (e % 2) * C : (e % 2 + 1) * C], lhsT=w, lhsT_scale=ws,
-                                    rhs=h_codes[e][:].bitcast(FP8X4), rhs_scale=h_scales[e][:], start=True, stop=True)
+                half = slice((e % 2) * C, (e % 2 + 1) * C)
+                nc.tensor.matmul_mx(bank[:, half], lhsT=w, lhsT_scale=ws, rhs=h_codes[pair][:, half].bitcast(FP8X4),
+                                    rhs_scale=h_scales[pair][:, half], start=True, stop=True)
             width = len(experts) * C
             dst = y[b][:, 2 * pair * C : 2 * pair * C + width]
             if u in Y_ON_VECTOR:
@@ -177,10 +179,18 @@ def tile_moe_hot_mlp_silu_kernel(
             else:
                 nc.scalar.copy(dst, bank[:, 0:width])
 
-        sum_bank = [1, 2, 3, 7, 6, 0]
-        back_bank = [4, 5]
+        sum_bank = [5, 2, 3, 7, 1, 4]
+        back_bank = [6, 0]
         first = [sb("first%d" % r, [P, T], F32) for r in range(TOP)]
-        ring = [[sb("ring%d_%d" % (j, r), [P, 2 * P], F32) for r in range(TOP)] for j in range(3)]
+        early = [sb("early%d" % r, [P, 4 * P], F32) for r in range(TOP)]
+        ring = [sb("ring%d" % r, [P, 4 * P], F32) for r in range(TOP)]
+
+        def product_tile(step, r, n):
+            if step < 2:
+                return early[r][:, step * 2 * P : step * 2 * P + n]
+            col = P if step == 2 else (step + 1) % 2 * 2 * P
+            return ring[r][:, col : col + n]
+
         out_codes = sb("out_codes", [P, T], I32)
         out_scales = sb("out_scales", [P, T], U8)
         out_rows = out_0.rearrange("(p t) k -> p t k", t=4)
@@ -200,32 +210,46 @@ def tile_moe_hot_mlp_silu_kernel(
             for r in range(TOP):
                 add_up(c, 0, r, first[r][:, c * P : (c + 1) * P])
 
+        last = T // P - 1
         for g, chunks in enumerate(TOKEN_GROUPS):
             t0, n = chunks[0] * P, len(chunks) * P
+            sums = [sb("sums%d" % c, [P, 4, P], F32) for c in chunks]
+
+            def sort_out(j, lo, hi):
+                src = banks[sum_bank[chunks[j]]][:, lo * P : hi * P].rearrange("k (p t) -> k t p", t=4)
+                nc.scalar.copy(sums[j][:, :, 32 * lo : 32 * hi], src)
+
             for b in range(1, 4):
-                slot = ring[(b - 1 - g) % 3]
+                if b == 3 and chunks[0] == last:
+                    sort_out(0, 0, 3)
                 for r in range(TOP):
-                    weigh(slot[r][:, 0:n], b, r, t0, n)
+                    product = product_tile(3 * g + b - 1, r, n)
+                    weigh(product, b, r, t0, n)
                     for j, c in enumerate(chunks):
-                        add_up(c, b, r, slot[r][:, j * P : (j + 1) * P])
-            result = sb("result%d" % g, [P, 4, n], F32)
-            rounded = sb("rounded%d" % g, [P, n, 4], BF16)
+                        add_up(c, b, r, product[:, j * P : (j + 1) * P])
+            group_rounded = sb("rounded%d" % g, [P, n, 4], BF16)
             for j, c in enumerate(chunks):
-                sums = sb("sums%d" % c, [P, 4, P], F32)
-                nc.scalar.copy(sums[:], banks[sum_bank[c]][:].rearrange("k (p t) -> k t p", t=4))
+                cols = slice(c * P, (c + 1) * P)
+                result = sb("result%d" % c, [P, 4, P], F32)
+                rounded = group_rounded[:, j * P : (j + 1) * P, :]
+                sort_out(j, 3 if c == last else 0, 4)
                 bank = banks[back_bank[c % 2]]
                 for t in range(4):
-                    nc.tensor.transpose(bank[:, t * P : (t + 1) * P], sums[:, t, :], ident[:])
+                    nc.tensor.transpose(bank[:, t * P : (t + 1) * P], sums[j][:, t, :], ident[:])
                 view = bank[:].rearrange("p (t k) -> p t k", t=4)
-                if len(chunks) == 2:
-                    nc.scalar.copy(result[:, :, j * P : (j + 1) * P], view)
-                    nc.scalar.copy(rounded[:, j * P : (j + 1) * P, :], view.rearrange("p t k -> p k t"))
+                if c == last:
+                    for half in (slice(0, P // 2), slice(P // 2, P)):
+                        nc.scalar.copy(result[:, :, half], view[:, :, half])
+                        nc.vector.tensor_copy(rounded[:, half, :].rearrange("p (a k) t -> p a t k", k=4),
+                                              result[:, :, half].rearrange("p t (a k) -> p a t k", k=4))
                 else:
-                    nc.vector.tensor_copy(rounded[:, j * P : (j + 1) * P, :], view.rearrange("p t k -> p k t"))
-                    nc.scalar.copy(result[:, :, j * P : (j + 1) * P], view)
-            nc.sync.dma_start(out_rows[:, :, t0 : t0 + n], result[:])
-            nc.vector.quantize_mx(out_codes[:, t0 : t0 + n].bitcast(FP8X4), out_scales[:, t0 : t0 + n],
-                                  rounded[:].rearrange("p k t -> p (k t)"))
-            nc.sync.dma_start(out_words[:, t0 : t0 + n], out_codes[:, t0 : t0 + n])
+                    nc.scalar.copy(result[:], view)
+                    nc.scalar.copy(rounded, view.rearrange("p t k -> p k t"))
+                nc.sync.dma_start(out_rows[:, :, cols], result[:])
+            cols = slice(t0, t0 + n)
+            nc.vector.quantize_mx(out_codes[:, cols].bitcast(FP8X4), out_scales[:, cols],
+                                  group_rounded[:].rearrange("p k t -> p (k t)"))
+            nc.sync.dma_start(out_words[:, cols], out_codes[:, cols])
         for r in range(4):
-            nc.sync.dma_start(out_2[0, r:16:4, :].bitcast(I32), out_scales[r:P:32, :].bitcast(I32))
+            queue = nc.sync if r % 2 == 0 else nc.scalar
+            queue.dma_start(out_2[0, r:16:4, :].bitcast(I32), out_scales[r:P:32, :].bitcast(I32))

@@ -181,7 +181,7 @@ def tile_moe_hot_mlp_silu_kernel(
 
         sum_bank = [5, 2, 3, 7, 1, 4]
         back_bank = [6, 0]
-        first = [sb("first%d" % r, [P, T], F32) for r in range(TOP)]
+        first = [sb("first%d" % r, [P, T - P], F32) for r in range(TOP)]
         early = [sb("early%d" % r, [P, 4 * P], F32) for r in range(TOP)]
         ring = [sb("ring%d" % r, [P, 4 * P], F32) for r in range(TOP)]
 
@@ -205,28 +205,30 @@ def tile_moe_hot_mlp_silu_kernel(
                              is_transpose=True, start=(r == 0), stop=(r == TOP - 1))
 
         for r in range(TOP):
-            weigh(first[r][:], 0, r, 0, T)
-        for c in range(T // P):
+            weigh(first[r][:], 0, r, 0, T - P)
+        for c in range(T // P - 1):
             for r in range(TOP):
                 add_up(c, 0, r, first[r][:, c * P : (c + 1) * P])
 
         last = T // P - 1
+        step = 0
         for g, chunks in enumerate(TOKEN_GROUPS):
             t0, n = chunks[0] * P, len(chunks) * P
             sums = [sb("sums%d" % c, [P, 4, P], F32) for c in chunks]
 
             def sort_out(j, lo, hi):
-                src = banks[sum_bank[chunks[j]]][:, lo * P : hi * P].rearrange("k (p t) -> k t p", t=4)
-                nc.scalar.copy(sums[j][:, :, 32 * lo : 32 * hi], src)
+                src = banks[sum_bank[chunks[j]]][:, lo * P : hi * P].rearrange("k (a p t) -> k a t p", p=4, t=4)
+                nc.scalar.copy(sums[j][:, :, 32 * lo : 32 * hi].rearrange("k t (a p) -> k a t p", p=4), src)
 
-            for b in range(1, 4):
+            for b in range(0 if chunks[0] == last else 1, 4):
                 if b == 3 and chunks[0] == last:
                     sort_out(0, 0, 3)
                 for r in range(TOP):
-                    product = product_tile(3 * g + b - 1, r, n)
+                    product = product_tile(step, r, n)
                     weigh(product, b, r, t0, n)
                     for j, c in enumerate(chunks):
                         add_up(c, b, r, product[:, j * P : (j + 1) * P])
+                step = step + 1
             group_rounded = sb("rounded%d" % g, [P, n, 4], BF16)
             for j, c in enumerate(chunks):
                 cols = slice(c * P, (c + 1) * P)

@@ -21,10 +21,10 @@ FP4X4 = mybir.dt.float4_e2m1fn_x4
 SILU = mybir.ActivationFunctionType.Silu
 MULT = mybir.AluOpType.mult
 
-SLOT_PIECES = [128, 128] + [256] * 7 + [128, 128]
-TOKEN_GROUPS = [(0, 1), (2, 3), (4,), (5,)]
-WORDS_ON_SCALAR = (3, 4, 5, 6, 7, 8)
-Y_ON_VECTOR = (2, 3)
+WORD_PIECES = [128, 128, 256, 512, 512, 512, 256]
+BYTE_PIECES = [256, 256, 512, 512, 512, 256]
+TURNS_ON_VECTOR = (4, 5, 6, 7)
+Y_ON_VECTOR = (2, 4)
 
 
 def tile_moe_hot_mlp_silu_kernel(
@@ -45,7 +45,10 @@ def tile_moe_hot_mlp_silu_kernel(
         pos_sb = [sb("pos_sb%d" % r, [P, T // 16], U16) for r in range(TOP)]
         xw = sb("xw", [P, T], I32)
         xs = sb("xs", [P, T], U8)
-        w1h_first = sb("w1h_first", [P, H], I32)
+        w1h_0 = sb("w1h_0", [P, H], I32)
+        w1h_1 = sb("w1h_1", [P, H], I32)
+        w1h_23 = sb("w1h_23", [P, 2, H], I32)
+        w1c = sb("w1c", [P, COLD, 2 * H], U8)
         s1h = sb("s1h", [P, H], U8)
         s2h = sb("s2h", [P, N], U8)
         s1c = sb("s1c", [P, COLD, H], U8)
@@ -54,10 +57,10 @@ def tile_moe_hot_mlp_silu_kernel(
         warm_in = sb("warm_in", [P, 1], F32)
         warm_out = sb("warm_out", [P, 1], F32)
 
-        nc.vector.memset(s1h[:].bitcast(I32), 0)
+        nc.gpsimd.memset(s1h[:].bitcast(I32), 0)
+        nc.gpsimd.memset(s1c[:].bitcast(I32), 0)
         nc.vector.memset(warm_in[:], 0.0)
         nc.scalar.activation(warm_out[:], warm_in[:], SILU)
-        nc.vector.memset(s1c[:].bitcast(I32), 0)
         nc.vector.memset(s2h[:].bitcast(I32), 0)
         nc.vector.memset(s2c[:].bitcast(I32), 0)
         make_identity(nc, ident[:])
@@ -76,99 +79,119 @@ def tile_moe_hot_mlp_silu_kernel(
         for r in range(4):
             nc.sync.dma_start(xs[32 * r : 32 * r + 32, :].bitcast(I32),
                               x_scales[0, 4 * r : 4 * r + 4, :].bitcast(I32).unsqueeze(0).to_broadcast([8, 4, T // 4]))
-        nc.sync.dma_start(xw[:], x_words[0].rearrange("p t d -> p (t d)").bitcast(I32))
         nc.sync.dma_start(offs_sb[:], offs)
-        nc.sync.dma_start(w1h_first[:], w1h_words[0, 0].rearrange("p c d -> p (c d)").bitcast(I32))
+        nc.sync.dma_start(xw[:], x_words[0].rearrange("p t d -> p (t d)").bitcast(I32))
+        nc.sync.dma_start(w1h_0[:], w1h_words[0, 0].rearrange("p c d -> p (c d)").bitcast(I32))
+        nc.sync.dma_start(pos_sb[0][:], pos1)
+        nc.sync.dma_start(pos_sb[1][:], pos2)
         load_hot_scales(s1h, w1h_scales)
-        w1h_rest = sb("w1h_rest", [P, HOT - 1, H], I32, tag="warm_in")
-        w1c = sb("w1c", [P, COLD, 2 * H], U8, tag="warm_out")
-        nc.sync.dma_start(w1h_rest[:], hot_words(w1h_words, 1, HOT))
+        nc.sync.dma_start(w1h_1[:], w1h_words[1, 0].rearrange("p c d -> p (c d)").bitcast(I32))
+        nc.sync.dma_start(w1h_23[:], hot_words(w1h_words, 2, HOT))
         load_cold_scales(s1c, w1c_scales)
         nc.sync.dma_start(w1c[:].bitcast(I32), w1c_words[:, 0].rearrange("e p b -> p e b").bitcast(I32))
         load_hot_scales(s2h, w2h_scales)
         load_cold_scales(s2c, w2c_scales)
-        for r, pos in enumerate((pos1, pos2, pos3)):
-            nc.sync.dma_start(pos_sb[r][:], pos)
+        nc.sync.dma_start(pos_sb[2][:], pos3)
 
-        chunk_words, chunk_scales = [], []
-        slot0 = 0
-        for j, n in enumerate(SLOT_PIECES):
-            piece = offs_sb[:, slot0 // 16 : (slot0 + n) // 16]
-            gw = sb("gw%d" % j, [P, n], U32)
-            gs = sb("gs%d" % j, [P, n], U8)
-            nc.vector.tensor_copy(gw[:], xw[:].bitcast(U32).indirect(piece))
-            nc.vector.tensor_copy(gs[:], xs[:].indirect(piece))
-            for c in range(n // P):
-                chunk_words.append(gw[:, c * P : (c + 1) * P])
-                chunk_scales.append(gs[:, c * P : (c + 1) * P])
-            slot0 = slot0 + n
-
-        h_rows = []
-        for k in range(S // P):
-            e = k * P // C
-            if e == 0:
-                w, ws = w1h_first[:].bitcast(FP8X4), s1h[:, :]
-            elif e < HOT:
-                w, ws = w1h_rest[:, e - 1, :].bitcast(FP8X4), s1h[4 * e : P, :]
-            else:
-                w, ws = w1c[:, e - HOT, :].bitcast(FP4X4), s1c[:, e - HOT, :]
-            bank = banks[k % 7]
-            nc.tensor.matmul_mx(bank[:], lhsT=chunk_words[k].bitcast(FP8X4), lhsT_scale=chunk_scales[k],
-                                rhs=w, rhs_scale=ws, start=True, stop=True)
-            rows = sb("h_rows%d" % k, [P, H], BF16)
-            nc.scalar.activation(rows[:].rearrange("s (u p e) -> s u p e", u=2, e=2),
-                                 bank[:].rearrange("s (p u e) -> s u p e", u=2, e=2), SILU)
-            h_rows.append(rows)
-
-        w2 = sb("w2", [P, HOT * 4 * N + COLD * 2 * N], U8, tag="w1h_first")
-        w2h = w2[:, 0 : HOT * 4 * N].bitcast(I32).rearrange("p (e c) -> p e c", e=HOT)
-        w2c = w2[:, HOT * 4 * N :].rearrange("p (e c) -> p e c", e=COLD)
-        nc.sync.dma_start(w2h, hot_words(w2h_words, 0, HOT))
-        nc.sync.dma_start(w2c.bitcast(I32), w2c_words[:, 0].rearrange("e p b -> p e b").bitcast(I32))
-
-        gate_sb = sb("gate_sb", [P, TOP, T], F32, tag="warm_in")
-        nc.sync.dma_start(gate_sb[:], gate.rearrange("r p t -> p r t"))
-
-        turn_bank = [7, 4, 5, 6, 0, 1, 2, 3, 7]
         pair_width = [min(2 * C, S - 2 * C * j) for j in range(5)]
         h_in = [sb("h_in%d" % j, [P, 4 * n], BF16) for j, n in enumerate(pair_width)]
         h_codes = [sb("h_codes%d" % j, [P, n], U32) for j, n in enumerate(pair_width)]
         h_scales = [sb("h_scales%d" % j, [P, n], U8) for j, n in enumerate(pair_width)]
+        h_rows = [sb("h_rows%d" % k, [P, H], BF16) for k in range(S // P)]
 
-        def turn(e):
-            bank = banks[turn_bank[e]]
-            for c in range(2):
-                words = h_rows[2 * e + c][:].bitcast(F32)
-                for u in range(2):
-                    col = (2 * c + u) * P
-                    nc.tensor.transpose(bank[:, col : col + P], words[:, u * P : (u + 1) * P], ident[:])
-            dst = h_in[e // 2][:, (e % 2) * 4 * C : (e % 2 + 1) * 4 * C].bitcast(F32).rearrange("p (c s u) -> p c s u", c=2, u=2)
-            src = bank[:].rearrange("p (c u s) -> p c s u", c=2, u=2)
-            if e in WORDS_ON_SCALAR:
-                nc.scalar.copy(dst, src)
+        def gather(name, window, dtype, pieces, j, ring):
+            slot0, n = sum(pieces[:j]), pieces[j]
+            dst = sb("%s%d" % (name, j), [P, n], dtype, tag="%s%d" % (name, j % ring))
+            nc.vector.tensor_copy(dst[:], window.indirect(offs_sb[:, slot0 // 16 : (slot0 + n) // 16]))
+            return [dst[:, c * P : (c + 1) * P] for c in range(n // P)]
+
+        def first_layer(k, words, scales):
+            e = k * P // C
+            if e < HOT:
+                w = (w1h_0[:], w1h_1[:], w1h_23[:, 0, :], w1h_23[:, 1, :])[e].bitcast(FP8X4)
+                ws = s1h[4 * e : P, :]
             else:
+                w, ws = w1c[:, e - HOT, :].bitcast(FP4X4), s1c[:, e - HOT, :]
+            bank = banks[k % 5]
+            nc.tensor.matmul_mx(bank[:], lhsT=words.bitcast(FP8X4), lhsT_scale=scales,
+                                rhs=w, rhs_scale=ws, start=True, stop=True)
+            nc.scalar.activation(h_rows[k][:].rearrange("s (u p e) -> s u p e", u=2, e=2),
+                                 bank[:].rearrange("s (p u e) -> s u p e", u=2, e=2), SILU)
+
+        def turn_place(k):
+            if k >= 16:
+                return banks[(7, 5)[k - 16]], 0
+            return banks[5 + (k // 2) % 3], (k % 2) * 2 * P
+
+        def turn(k):
+            bank, col = turn_place(k)
+            words = h_rows[k][:].bitcast(F32)
+            for u in range(2):
+                nc.tensor.transpose(bank[:, col + u * P : col + (u + 1) * P], words[:, u * P : (u + 1) * P], ident[:])
+
+        def weave(k0, count, on_vector):
+            bank, col = turn_place(k0)
+            at = (k0 % 4) * 4 * P
+            dst = h_in[k0 // 4][:, at : at + count * 4 * P].bitcast(F32).rearrange("p (c s u) -> p c s u", c=count, u=2)
+            src = bank[:, col : col + count * 2 * P].rearrange("p (c u s) -> p c s u", c=count, u=2)
+            if on_vector:
                 nc.vector.tensor_copy(dst, src)
+            else:
+                nc.scalar.copy(dst, src)
 
-        def quantise(e):
-            nc.vector.quantize_mx(h_codes[e][:].bitcast(FP8X4), h_scales[e][:], h_in[e][:])
+        def quantise(j):
+            nc.vector.quantize_mx(h_codes[j][:].bitcast(FP8X4), h_scales[j][:], h_in[j][:])
 
-        for e in range(E):
-            turn(e)
-            if e >= 2 and e % 2 == 0:
-                quantise(e // 2 - 1)
-        quantise(E // 2)
+        chunk_words, chunk_scales = [], []
+        word_piece = byte_piece = 0
+        for k in range(S // P):
+            if k == len(chunk_scales):
+                chunk_scales.extend(gather("gs", xs[:], U8, BYTE_PIECES, byte_piece, 2))
+                byte_piece = byte_piece + 1
+            if k == len(chunk_words):
+                chunk_words.extend(gather("gw", xw[:].bitcast(U32), U32, WORD_PIECES, word_piece, 3))
+                word_piece = word_piece + 1
+            first_layer(k, chunk_words[k], chunk_scales[k])
+            e = k // 2
+            if k >= 16:
+                turn(k)
+            elif k % 2 == 1:
+                turn(k - 1)
+                turn(k)
+                if e in TURNS_ON_VECTOR:
+                    weave(k - 1, 2, True)
+                if e >= 2 and e - 2 not in TURNS_ON_VECTOR:
+                    weave(2 * (e - 2), 2, False)
+                if e in (3, 5, 7):
+                    quantise(e // 2 - 1 if e == 3 else e // 2)
+                if e == 5:
+                    quantise(1)
+        weave(16, 1, False)
+        weave(17, 1, False)
+        quantise(4)
+
+        w2h_words_i = hot_words(w2h_words, 0, HOT)
+        w2c_words_i = w2c_words[:, 0].rearrange("e p b -> p e b").bitcast(I32)
+        w2h = [sb("w2h_first", [P, HOT, P], I32), sb("w2h_rest", [P, HOT, N - P], I32, tag="w1h_0")]
+        w2c = [sb("w2c_first", [P, COLD, P // 2], I32), sb("w2c_rest", [P, COLD, (N - P) // 2], I32, tag="w1h_1")]
+        nc.sync.dma_start(w2h[0][:], w2h_words_i[:, :, 0:P])
+        nc.sync.dma_start(w2c[0][:], w2c_words_i[:, :, 0 : P // 2])
+        gate_sb = sb("gate_sb", [P, TOP, T], F32, tag="warm_in")
+        nc.sync.dma_start(gate_sb[:], gate.rearrange("r p t -> p r t"))
+        nc.sync.dma_start(w2h[1][:], w2h_words_i[:, :, P:N])
+        nc.sync.dma_start(w2c[1][:], w2c_words_i[:, :, P // 2 : N // 2])
 
         y = [sb("y%d" % b, [P, S], F32) for b in range(4)]
-        second_bank = [6, 0, 1, 4, 5, 2, 3, 7]
         for u in range(20):
             b, pair = divmod(u, 5)
-            bank = banks[second_bank[u % 8]]
+            bank = banks[(3, 4, 0, 1, 2)[u]] if b == 0 else banks[((5, 4, 0, 3, 6) if b == 1 else (1, 2, 5, 4, 0))[pair]]
+            at = max(b - 1, 0) * P
             experts = range(2 * pair, min(2 * pair + 2, E))
             for e in experts:
                 if e < HOT:
-                    w, ws = w2h[:, e, b * P : (b + 1) * P].bitcast(FP8X4), s2h[4 * e : P, b * P : (b + 1) * P]
+                    w, ws = w2h[min(b, 1)][:, e, at : at + P].bitcast(FP8X4), s2h[4 * e : P, b * P : (b + 1) * P]
                 else:
-                    w, ws = w2c[:, e - HOT, 2 * b * P : 2 * (b + 1) * P].bitcast(FP4X4), s2c[:, e - HOT, b * P : (b + 1) * P]
+                    w, ws = w2c[min(b, 1)][:, e - HOT, at // 2 : (at + P) // 2].bitcast(U8).bitcast(FP4X4), s2c[:, e - HOT, b * P : (b + 1) * P]
                 half = slice((e % 2) * C, (e % 2 + 1) * C)
                 nc.tensor.matmul_mx(bank[:, half], lhsT=w, lhsT_scale=ws, rhs=h_codes[pair][:, half].bitcast(FP8X4),
                                     rhs_scale=h_scales[pair][:, half], start=True, stop=True)
@@ -179,79 +202,113 @@ def tile_moe_hot_mlp_silu_kernel(
             else:
                 nc.scalar.copy(dst, bank[:, 0:width])
 
-        sum_bank = [5, 2, 3, 7, 1, 4]
-        back_bank = [6, 0]
-        first = [sb("first%d" % r, [P, T - P], F32) for r in range(TOP)]
-        early = [sb("early%d" % r, [P, 4 * P], F32) for r in range(TOP)]
-        ring = [sb("ring%d" % r, [P, 4 * P], F32) for r in range(TOP)]
-
-        def product_tile(step, r, n):
-            if step < 2:
-                return early[r][:, step * 2 * P : step * 2 * P + n]
-            col = P if step == 2 else (step + 1) % 2 * 2 * P
-            return ring[r][:, col : col + n]
-
-        out_codes = sb("out_codes", [P, T], I32)
-        out_scales = sb("out_scales", [P, T], U8)
+        back_bank = [3, 6, 1, 2, 5]
+        first = [sb("first%d" % r, [P, 4 * P], F32) for r in range(TOP)]
+        ring = [sb("ring%d" % r, [P, 5 * P], F32) for r in range(TOP)]
         out_rows = out_0.rearrange("(p t) k -> p t k", t=4)
+        out_blocks = out_0.rearrange("(b p) k -> p b k", p=P)
         out_words = out_1[0].rearrange("p t d -> p (t d)").bitcast(I32)
+        rounded = [sb("rounded0", [P, 3 * P, 4], BF16)]
+        results = []
 
-        def weigh(dst, b, r, t0, n):
-            nc.vector.tensor_tensor(dst, y[b][:].indirect(pos_sb[r][:, t0 // 16 : (t0 + n) // 16]),
-                                    gate_sb[:, r, t0 : t0 + n], MULT)
-
-        def add_up(c, b, r, src):
-            nc.tensor.matmul(banks[sum_bank[c]][:, b * P : (b + 1) * P], lhsT=src, rhs=ident[:],
-                             is_transpose=True, start=(r == 0), stop=(r == TOP - 1))
-
-        for r in range(TOP):
-            weigh(first[r][:], 0, r, 0, T - P)
-        for c in range(T // P - 1):
+        def combine(tiles, col, b, c0, count, targets):
             for r in range(TOP):
-                add_up(c, 0, r, first[r][:, c * P : (c + 1) * P])
+                product = tiles[r][:, col : col + count * P]
+                t0 = c0 * P
+                nc.vector.tensor_tensor(product, y[b][:].indirect(pos_sb[r][:, t0 // 16 : (t0 + count * P) // 16]),
+                                        gate_sb[:, r, t0 : t0 + count * P], MULT)
+            for j in range(count):
+                for r in range(TOP):
+                    nc.tensor.matmul(targets[j], lhsT=tiles[r][:, col + j * P : col + (j + 1) * P], rhs=ident[:],
+                                     is_transpose=True, start=(r == 0), stop=(r == TOP - 1))
+
+        def pair_bank(c0, half):
+            return banks[7] if half == 1 else banks[back_bank[c0 // 2]]
+
+        def pair_places(c0, b):
+            return [pair_bank(c0, b // 2)[:, (2 * j + b % 2) * P : (2 * j + b % 2 + 1) * P] for j in range(2)]
+
+        sums = [sb("sums%d" % g, [P, n, 4, P], F32) for g, n in enumerate((2, 2, 1))]
+
+        def sort_pair(c0, half):
+            nc.scalar.copy(sums[c0 // 2][:, :, :, 64 * half : 64 * half + 64].rearrange("k c t (a p) -> k c a t p", p=4),
+                           pair_bank(c0, half)[:].rearrange("k (c a p t) -> k c a t p", c=2, p=4, t=4))
+
+        def turn_back(c):
+            bank = banks[back_bank[c]]
+            for t in range(4):
+                nc.tensor.transpose(bank[:, t * P : (t + 1) * P], sums[c // 2][:, c % 2, t, :], ident[:])
+            view = bank[:].rearrange("p (t k) -> p t k", t=4)
+            result = sb("result%d" % c, [P, 4, P], F32)
+            nc.scalar.copy(result[:], view)
+            results.append(result)
+            if c < 3:
+                nc.scalar.copy(rounded[0][:, c * P : (c + 1) * P, :], view.rearrange("p t k -> p k t"))
+            nc.sync.dma_start(out_rows[:, :, c * P : (c + 1) * P], result[:])
+
+        combine(first, 0, 0, 0, 4, pair_places(0, 0) + pair_places(2, 0))
+        combine(ring, P, 1, 0, 4, pair_places(0, 1) + pair_places(2, 1))
+        sort_pair(0, 0)
+        sort_pair(2, 0)
+        for tiles, col, b, c0 in ((first, 0, 2, 0), (ring, P, 3, 0), (ring, 3 * P, 3, 2), (ring, 0, 2, 2)):
+            combine(tiles, col, b, c0, 2, pair_places(c0, b))
+            if (b, c0) in ((3, 0), (2, 2)):
+                sort_pair(c0, 1)
+                turn_back(c0)
+                turn_back(c0 + 1)
+        for half in range(2):
+            bank = banks[(4, 7)[half]]
+            for b in (2 * half, 2 * half + 1):
+                combine(ring, (2 + b) % 5 * P, b, 4, 1, [bank[:, (b % 2) * P : (b % 2 + 1) * P]])
+            nc.scalar.copy(sums[2][:, 0, :, 64 * half : 64 * half + 64].rearrange("k t (a p) -> k a t p", p=4),
+                           bank[:, 0 : 2 * P].rearrange("k (a p t) -> k a t p", p=4, t=4))
+        turn_back(4)
 
         last = T // P - 1
-        step = 0
-        for g, chunks in enumerate(TOKEN_GROUPS):
-            t0, n = chunks[0] * P, len(chunks) * P
-            sums = [sb("sums%d" % c, [P, 4, P], F32) for c in chunks]
+        cols = slice(last * P, T)
+        half_bank = [banks[back_bank[2]], banks[7]]
+        pairs = sb("pairs", [P, 2, P, 2], BF16)
+        plain = sb("plain", [P, 4 * P], F32)
+        for half in range(2):
+            for b in (2 * half, 2 * half + 1):
+                combine(ring, (1 + b) * P, b, last, 1, [half_bank[half][:, (b % 2) * P : (b % 2 + 1) * P]])
+            src = half_bank[half][:, 0 : 2 * P]
+            nc.scalar.copy(pairs[:, :, half * 64 : half * 64 + 64, :], src.rearrange("k (p u e) -> k u p e", u=2, e=2))
+            nc.scalar.copy(plain[:, half * 2 * P : (half + 1) * 2 * P], src)
+        pair_words = pairs[:].rearrange("k u p e -> k (u p e)").bitcast(F32)
+        for u in range(2):
+            nc.tensor.transpose(banks[3][:, u * P : (u + 1) * P], pair_words[:, u * P : (u + 1) * P], ident[:])
+        last_result = sb("last_result", [P, 4, P], F32)
+        for half in range(2):
+            bank = banks[(6, 0)[half]]
+            for j in range(2):
+                b = 2 * half + j
+                nc.tensor.transpose(bank[:, j * P : (j + 1) * P], plain[:, b * P : (b + 1) * P], ident[:])
+            part = last_result[:, 2 * half : 2 * half + 2, :]
+            nc.scalar.copy(part, bank[:, 0 : 2 * P].rearrange("p (b k) -> p b k", b=2))
+            nc.sync.dma_start(out_blocks[:, 2 * half : 2 * half + 2, cols], part)
 
-            def sort_out(j, lo, hi):
-                src = banks[sum_bank[chunks[j]]][:, lo * P : hi * P].rearrange("k (a p t) -> k a t p", p=4, t=4)
-                nc.scalar.copy(sums[j][:, :, 32 * lo : 32 * hi].rearrange("k t (a p) -> k a t p", p=4), src)
+        out_codes = sb("out_codes", [P, T], I32, tag="warm_in")
+        out_scales = sb("out_scales", [P, T], U8)
 
-            for b in range(0 if chunks[0] == last else 1, 4):
-                if b == 3 and chunks[0] == last:
-                    sort_out(0, 0, 3)
-                for r in range(TOP):
-                    product = product_tile(step, r, n)
-                    weigh(product, b, r, t0, n)
-                    for j, c in enumerate(chunks):
-                        add_up(c, b, r, product[:, j * P : (j + 1) * P])
-                step = step + 1
-            group_rounded = sb("rounded%d" % g, [P, n, 4], BF16)
-            for j, c in enumerate(chunks):
-                cols = slice(c * P, (c + 1) * P)
-                result = sb("result%d" % c, [P, 4, P], F32)
-                rounded = group_rounded[:, j * P : (j + 1) * P, :]
-                sort_out(j, 3 if c == last else 0, 4)
-                bank = banks[back_bank[c % 2]]
-                for t in range(4):
-                    nc.tensor.transpose(bank[:, t * P : (t + 1) * P], sums[j][:, t, :], ident[:])
-                view = bank[:].rearrange("p (t k) -> p t k", t=4)
-                if c == last:
-                    for half in (slice(0, P // 2), slice(P // 2, P)):
-                        nc.scalar.copy(result[:, :, half], view[:, :, half])
-                        nc.vector.tensor_copy(rounded[:, half, :].rearrange("p (a k) t -> p a t k", k=4),
-                                              result[:, :, half].rearrange("p t (a k) -> p a t k", k=4))
-                else:
-                    nc.scalar.copy(result[:], view)
-                    nc.scalar.copy(rounded, view.rearrange("p t k -> p k t"))
-                nc.sync.dma_start(out_rows[:, :, cols], result[:])
-            cols = slice(t0, t0 + n)
-            nc.vector.quantize_mx(out_codes[:, cols].bitcast(FP8X4), out_scales[:, cols],
-                                  group_rounded[:].rearrange("p k t -> p (k t)"))
-            nc.sync.dma_start(out_words[:, cols], out_codes[:, cols])
+        rounded.append(sb("rounded1", [P, 2 * P, 4], BF16, tag="y3"))
+        rounded.append(sb("rounded2", [P, P, 4], BF16))
+
+        def quantise_out(g, at, t0, n):
+            nc.vector.quantize_mx(out_codes[:, t0 : t0 + n].bitcast(FP8X4), out_scales[:, t0 : t0 + n],
+                                  rounded[g][:, at : at + n, :].rearrange("p k t -> p (k t)"))
+
+        for c in (3, 4):
+            nc.vector.tensor_copy(rounded[1][:, (c - 3) * P : (c - 2) * P, :].rearrange("p (a k) t -> p a t k", k=4),
+                                  results[c][:].rearrange("p t (a k) -> p a t k", k=4))
+        quantise_out(0, 0, 0, 2 * P)
+        quantise_out(0, 2 * P, 2 * P, P)
+        quantise_out(1, 0, 3 * P, 2 * P)
+        nc.sync.dma_start(out_words[:, 0 : last * P], out_codes[:, 0 : last * P])
+        nc.vector.tensor_copy(rounded[2][:].rearrange("p k t -> p (k t)").bitcast(F32).rearrange("p (k u) -> p k u", u=2),
+                              banks[3][:, 0 : 2 * P].rearrange("p (u k) -> p k u", u=2))
+        quantise_out(2, 0, last * P, P)
+        nc.sync.dma_start(out_words[:, cols], out_codes[:, cols])
         for r in range(4):
             queue = nc.sync if r % 2 == 0 else nc.scalar
             queue.dma_start(out_2[0, r:16:4, :].bitcast(I32), out_scales[r:P:32, :].bitcast(I32))

@@ -21,8 +21,8 @@ FP4X4 = mybir.dt.float4_e2m1fn_x4
 SILU = mybir.ActivationFunctionType.Silu
 MULT = mybir.AluOpType.mult
 
-WORD_PIECES = [128, 128, 256, 512, 512, 512, 256]
-BYTE_PIECES = [256, 256, 512, 512, 512, 256]
+WORD_PIECES = [128, 128, 256, 256, 512, 512, 512]
+BYTE_PIECES = [256, 256, 256, 512, 512, 512]
 TURNS_ON_VECTOR = (4, 5, 6, 7)
 Y_ON_VECTOR = (2, 4)
 
@@ -57,7 +57,7 @@ def tile_moe_hot_mlp_silu_kernel(
         warm_in = sb("warm_in", [P, 1], F32)
         warm_out = sb("warm_out", [P, 1], F32)
 
-        nc.gpsimd.memset(s1h[:].bitcast(I32), 0)
+        nc.vector.memset(s1h[:].bitcast(I32), 0)
         nc.gpsimd.memset(s1c[:].bitcast(I32), 0)
         nc.vector.memset(warm_in[:], 0.0)
         nc.scalar.activation(warm_out[:], warm_in[:], SILU)
@@ -82,8 +82,6 @@ def tile_moe_hot_mlp_silu_kernel(
         nc.sync.dma_start(offs_sb[:], offs)
         nc.sync.dma_start(xw[:], x_words[0].rearrange("p t d -> p (t d)").bitcast(I32))
         nc.sync.dma_start(w1h_0[:], w1h_words[0, 0].rearrange("p c d -> p (c d)").bitcast(I32))
-        nc.sync.dma_start(pos_sb[0][:], pos1)
-        nc.sync.dma_start(pos_sb[1][:], pos2)
         load_hot_scales(s1h, w1h_scales)
         nc.sync.dma_start(w1h_1[:], w1h_words[1, 0].rearrange("p c d -> p (c d)").bitcast(I32))
         nc.sync.dma_start(w1h_23[:], hot_words(w1h_words, 2, HOT))
@@ -91,7 +89,8 @@ def tile_moe_hot_mlp_silu_kernel(
         nc.sync.dma_start(w1c[:].bitcast(I32), w1c_words[:, 0].rearrange("e p b -> p e b").bitcast(I32))
         load_hot_scales(s2h, w2h_scales)
         load_cold_scales(s2c, w2c_scales)
-        nc.sync.dma_start(pos_sb[2][:], pos3)
+        for r, pos in enumerate((pos1, pos2, pos3)):
+            nc.sync.dma_start(pos_sb[r][:], pos)
 
         pair_width = [min(2 * C, S - 2 * C * j) for j in range(5)]
         h_in = [sb("h_in%d" % j, [P, 4 * n], BF16) for j, n in enumerate(pair_width)]
@@ -162,10 +161,8 @@ def tile_moe_hot_mlp_silu_kernel(
                     weave(k - 1, 2, True)
                 if e >= 2 and e - 2 not in TURNS_ON_VECTOR:
                     weave(2 * (e - 2), 2, False)
-                if e in (3, 5, 7):
-                    quantise(e // 2 - 1 if e == 3 else e // 2)
-                if e == 5:
-                    quantise(1)
+                for j in {3: (0,), 5: (1, 2), 7: (3,)}.get(e, ()):
+                    quantise(j)
         weave(16, 1, False)
         weave(17, 1, False)
         quantise(4)
@@ -184,7 +181,7 @@ def tile_moe_hot_mlp_silu_kernel(
         y = [sb("y%d" % b, [P, S], F32) for b in range(4)]
         for u in range(20):
             b, pair = divmod(u, 5)
-            bank = banks[(3, 4, 0, 1, 2)[u]] if b == 0 else banks[((5, 4, 0, 3, 6) if b == 1 else (1, 2, 5, 4, 0))[pair]]
+            bank = banks[(3, 4, 0, 1, 2)[u]] if b == 0 else banks[(5, 0, 4, 3, 6)[pair] if b == 1 else (1, 2, 5, 0)[(u - 10) % 4]]
             at = max(b - 1, 0) * P
             experts = range(2 * pair, min(2 * pair + 2, E))
             for e in experts:
@@ -203,7 +200,7 @@ def tile_moe_hot_mlp_silu_kernel(
                 nc.scalar.copy(dst, bank[:, 0:width])
 
         back_bank = [3, 6, 1, 2, 5]
-        first = [sb("first%d" % r, [P, 4 * P], F32) for r in range(TOP)]
+        first = [sb("first%d" % r, [P, 5 * P], F32) for r in range(TOP)]
         ring = [sb("ring%d" % r, [P, 5 * P], F32) for r in range(TOP)]
         out_rows = out_0.rearrange("(p t) k -> p t k", t=4)
         out_blocks = out_0.rearrange("(b p) k -> p b k", p=P)
@@ -246,22 +243,24 @@ def tile_moe_hot_mlp_silu_kernel(
                 nc.scalar.copy(rounded[0][:, c * P : (c + 1) * P, :], view.rearrange("p t k -> p k t"))
             nc.sync.dma_start(out_rows[:, :, c * P : (c + 1) * P], result[:])
 
-        combine(first, 0, 0, 0, 4, pair_places(0, 0) + pair_places(2, 0))
-        combine(ring, P, 1, 0, 4, pair_places(0, 1) + pair_places(2, 1))
+        def sort_single(bank, half):
+            nc.scalar.copy(sums[2][:, 0, :, 64 * half : 64 * half + 64].rearrange("k t (a p) -> k a t p", p=4),
+                           bank[:, 0 : 2 * P].rearrange("k (a p t) -> k a t p", p=4, t=4))
+
+        for b, tiles in enumerate((first, ring)):
+            combine(tiles, 0, b, 0, 5, pair_places(0, b) + pair_places(2, b) + [banks[4][:, b * P : (b + 1) * P]])
         sort_pair(0, 0)
         sort_pair(2, 0)
-        for tiles, col, b, c0 in ((first, 0, 2, 0), (ring, P, 3, 0), (ring, 3 * P, 3, 2), (ring, 0, 2, 2)):
+        sort_single(banks[4], 0)
+        for tiles, col, b, c0 in ((first, 0, 2, 0), (first, 2 * P, 3, 0), (ring, 3 * P, 3, 2), (first, P, 2, 2)):
             combine(tiles, col, b, c0, 2, pair_places(c0, b))
             if (b, c0) in ((3, 0), (2, 2)):
                 sort_pair(c0, 1)
                 turn_back(c0)
                 turn_back(c0 + 1)
-        for half in range(2):
-            bank = banks[(4, 7)[half]]
-            for b in (2 * half, 2 * half + 1):
-                combine(ring, (2 + b) % 5 * P, b, 4, 1, [bank[:, (b % 2) * P : (b % 2 + 1) * P]])
-            nc.scalar.copy(sums[2][:, 0, :, 64 * half : 64 * half + 64].rearrange("k t (a p) -> k a t p", p=4),
-                           bank[:, 0 : 2 * P].rearrange("k (a p t) -> k a t p", p=4, t=4))
+        for b, tiles in ((2, first), (3, ring)):
+            combine(tiles, 3 * P, b, 4, 1, [banks[7][:, (b % 2) * P : (b % 2 + 1) * P]])
+        sort_single(banks[7], 1)
         turn_back(4)
 
         last = T // P - 1
@@ -271,7 +270,7 @@ def tile_moe_hot_mlp_silu_kernel(
         plain = sb("plain", [P, 4 * P], F32)
         for half in range(2):
             for b in (2 * half, 2 * half + 1):
-                combine(ring, (1 + b) * P, b, last, 1, [half_bank[half][:, (b % 2) * P : (b % 2 + 1) * P]])
+                combine(first if b else ring, (b or 4) * P, b, last, 1, [half_bank[half][:, (b % 2) * P : (b % 2 + 1) * P]])
             src = half_bank[half][:, 0 : 2 * P]
             nc.scalar.copy(pairs[:, :, half * 64 : half * 64 + 64, :], src.rearrange("k (p u e) -> k u p e", u=2, e=2))
             nc.scalar.copy(plain[:, half * 2 * P : (half + 1) * 2 * P], src)
@@ -308,7 +307,7 @@ def tile_moe_hot_mlp_silu_kernel(
         nc.vector.tensor_copy(rounded[2][:].rearrange("p k t -> p (k t)").bitcast(F32).rearrange("p (k u) -> p k u", u=2),
                               banks[3][:, 0 : 2 * P].rearrange("p (u k) -> p k u", u=2))
         quantise_out(2, 0, last * P, P)
-        nc.sync.dma_start(out_words[:, cols], out_codes[:, cols])
+        nc.scalar.dma_start(out_words[:, cols], out_codes[:, cols])
         for r in range(4):
             queue = nc.sync if r % 2 == 0 else nc.scalar
             queue.dma_start(out_2[0, r:16:4, :].bitcast(I32), out_scales[r:P:32, :].bitcast(I32))

@@ -21,10 +21,10 @@ FP4X4 = mybir.dt.float4_e2m1fn_x4
 SILU = mybir.ActivationFunctionType.Silu
 MULT = mybir.AluOpType.mult
 
-WORD_PIECES = [128, 128, 256, 256, 512, 512, 512]
-BYTE_PIECES = [256, 256, 256, 512, 512, 512]
-TURNS_ON_VECTOR = (4, 5, 6, 7)
-Y_ON_VECTOR = (2, 4)
+WORD_PIECES = [(128, None), (128, None), (256, None), (256, None), (512, "gs0"), (512, "gs1"), (512, "gw3")]
+BYTE_PIECES = [(256, None), (256, None), (256, "gw0"), (512, "gw1"), (512, "gw2"), (512, "w1c_a")]
+UNITS = ((4, 5), (6, 7), (0, 1), (2, 3), (8,))
+Y_ON_VECTOR = (3, 4)
 
 
 def tile_moe_hot_mlp_silu_kernel(
@@ -45,10 +45,11 @@ def tile_moe_hot_mlp_silu_kernel(
         pos_sb = [sb("pos_sb%d" % r, [P, T // 16], U16) for r in range(TOP)]
         xw = sb("xw", [P, T], I32)
         xs = sb("xs", [P, T], U8)
-        w1h_0 = sb("w1h_0", [P, H], I32)
-        w1h_1 = sb("w1h_1", [P, H], I32)
-        w1h_23 = sb("w1h_23", [P, 2, H], I32)
-        w1c = sb("w1c", [P, COLD, 2 * H], U8)
+        w1h = [sb("w1h_%d" % j, [P, 2, H], I32) for j in range(2)]
+        w1c_a = sb("w1c_a", [P, 2, 2 * H], U8)
+        w1c_b = sb("w1c_b", [P, 3, 2 * H], U8)
+        w1_dealt = [sb("w1_dealt%d" % e, [P, H], I32) for e in range(HOT)]
+        s1_dealt = sb("s1_dealt", [P, H], U8)
         s1h = sb("s1h", [P, H], U8)
         s2h = sb("s2h", [P, N], U8)
         s1c = sb("s1c", [P, COLD, H], U8)
@@ -57,8 +58,8 @@ def tile_moe_hot_mlp_silu_kernel(
         warm_in = sb("warm_in", [P, 1], F32)
         warm_out = sb("warm_out", [P, 1], F32)
 
+        nc.vector.memset(s1c[:].bitcast(I32), 0)
         nc.vector.memset(s1h[:].bitcast(I32), 0)
-        nc.gpsimd.memset(s1c[:].bitcast(I32), 0)
         nc.vector.memset(warm_in[:], 0.0)
         nc.scalar.activation(warm_out[:], warm_in[:], SILU)
         nc.vector.memset(s2h[:].bitcast(I32), 0)
@@ -81,125 +82,135 @@ def tile_moe_hot_mlp_silu_kernel(
                               x_scales[0, 4 * r : 4 * r + 4, :].bitcast(I32).unsqueeze(0).to_broadcast([8, 4, T // 4]))
         nc.sync.dma_start(offs_sb[:], offs)
         nc.sync.dma_start(xw[:], x_words[0].rearrange("p t d -> p (t d)").bitcast(I32))
-        nc.sync.dma_start(w1h_0[:], w1h_words[0, 0].rearrange("p c d -> p (c d)").bitcast(I32))
-        load_hot_scales(s1h, w1h_scales)
-        nc.sync.dma_start(w1h_1[:], w1h_words[1, 0].rearrange("p c d -> p (c d)").bitcast(I32))
-        nc.sync.dma_start(w1h_23[:], hot_words(w1h_words, 2, HOT))
+        nc.sync.dma_start(w1c_a[:].bitcast(I32), w1c_words[0:2, 0].rearrange("e p b -> p e b").bitcast(I32))
         load_cold_scales(s1c, w1c_scales)
-        nc.sync.dma_start(w1c[:].bitcast(I32), w1c_words[:, 0].rearrange("e p b -> p e b").bitcast(I32))
-        load_hot_scales(s2h, w2h_scales)
+        nc.sync.dma_start(w1c_b[:].bitcast(I32), w1c_words[2:COLD, 0].rearrange("e p b -> p e b").bitcast(I32))
+        load_hot_scales(s1h, w1h_scales)
+        for j in range(2):
+            nc.sync.dma_start(w1h[j][:], hot_words(w1h_words, 2 * j, 2 * j + 2))
+
+        def deal(dst, src):
+            nc.gpsimd.tensor_copy(dst.rearrange("p (t m) -> p t m", t=4), src.rearrange("p (m t) -> p t m", t=4))
+
+        deal(s1_dealt[:], s1h[:])
+        for e in range(HOT):
+            deal(w1_dealt[e][:], w1h[e // 2][:, e % 2, :])
+
+        w2h_words_i = hot_words(w2h_words, 0, HOT)
+        w2c_words_i = w2c_words[:, 0].rearrange("e p b -> p e b").bitcast(I32)
+        w2h = [sb("w2h_first", [P, HOT, P], I32)]
+        w2c = [sb("w2c_first", [P, COLD, P // 2], I32)]
         load_cold_scales(s2c, w2c_scales)
+        nc.sync.dma_start(w2c[0][:], w2c_words_i[:, :, 0 : P // 2])
+        load_hot_scales(s2h, w2h_scales)
+        nc.sync.dma_start(w2h[0][:], w2h_words_i[:, :, 0:P])
         for r, pos in enumerate((pos1, pos2, pos3)):
             nc.sync.dma_start(pos_sb[r][:], pos)
 
-        pair_width = [min(2 * C, S - 2 * C * j) for j in range(5)]
-        h_in = [sb("h_in%d" % j, [P, 4 * n], BF16) for j, n in enumerate(pair_width)]
-        h_codes = [sb("h_codes%d" % j, [P, n], U32) for j, n in enumerate(pair_width)]
-        h_scales = [sb("h_scales%d" % j, [P, n], U8) for j, n in enumerate(pair_width)]
-        h_rows = [sb("h_rows%d" % k, [P, H], BF16) for k in range(S // P)]
+        h_in = [sb("h_in%d" % j, [P, 4 * C * len(unit)], BF16) for j, unit in enumerate(UNITS)]
+        h_scales = [sb("h_scales%d" % j, [P, C * len(unit)], U8) for j, unit in enumerate(UNITS)]
+        h_rows = [sb("h_rows%d" % k, [P, H], BF16) for k in range(2 * COLD)]
+        h_codes = {}
 
-        def gather(name, window, dtype, pieces, j, ring):
-            slot0, n = sum(pieces[:j]), pieces[j]
-            dst = sb("%s%d" % (name, j), [P, n], dtype, tag="%s%d" % (name, j % ring))
+        def h_place(e):
+            j = [e in unit for unit in UNITS].index(True)
+            at = UNITS[j].index(e) * 4 * C
+            return h_in[j][:, at : at + 4 * C]
+
+        def gather(name, window, dtype, pieces, j):
+            slot0, (n, tag) = (HOT * C + sum(piece[0] for piece in pieces[:j])) % S, pieces[j]
+            dst = sb("%s%d" % (name, j), [P, n], dtype, tag=tag)
             nc.vector.tensor_copy(dst[:], window.indirect(offs_sb[:, slot0 // 16 : (slot0 + n) // 16]))
             return [dst[:, c * P : (c + 1) * P] for c in range(n // P)]
 
         def first_layer(k, words, scales):
-            e = k * P // C
+            e = (k // 2 + HOT) % E
+            bank = banks[k % 4]
             if e < HOT:
-                w = (w1h_0[:], w1h_1[:], w1h_23[:, 0, :], w1h_23[:, 1, :])[e].bitcast(FP8X4)
-                ws = s1h[4 * e : P, :]
-            else:
-                w, ws = w1c[:, e - HOT, :].bitcast(FP4X4), s1c[:, e - HOT, :]
-            bank = banks[k % 5]
+                for t in range(4):
+                    cols = slice(t * P, (t + 1) * P)
+                    nc.tensor.matmul_mx(bank[:, cols], lhsT=w1_dealt[e][:, cols].bitcast(FP8X4), lhsT_scale=s1_dealt[4 * e : P, cols],
+                                        rhs=words.bitcast(FP8X4), rhs_scale=scales, start=True, stop=True)
+                at = (k % 2) * 4 * P
+                nc.scalar.activation(h_place(e)[:, at : at + 4 * P].rearrange("p (s t) -> p s t", t=4),
+                                     bank[:].rearrange("p (t s) -> p s t", t=4), SILU)
+                return
+            c = e - HOT
+            w, ws = (w1c_a[:, c, :] if c < 2 else w1c_b[:, c - 2, :]).bitcast(FP4X4), s1c[:, c, :]
             nc.tensor.matmul_mx(bank[:], lhsT=words.bitcast(FP8X4), lhsT_scale=scales,
                                 rhs=w, rhs_scale=ws, start=True, stop=True)
             nc.scalar.activation(h_rows[k][:].rearrange("s (u p e) -> s u p e", u=2, e=2),
                                  bank[:].rearrange("s (p u e) -> s u p e", u=2, e=2), SILU)
 
-        def turn_place(k):
-            if k >= 16:
-                return banks[(7, 5)[k - 16]], 0
-            return banks[5 + (k // 2) % 3], (k % 2) * 2 * P
-
-        def turn(k):
-            bank, col = turn_place(k)
-            words = h_rows[k][:].bitcast(F32)
-            for u in range(2):
-                nc.tensor.transpose(bank[:, col + u * P : col + (u + 1) * P], words[:, u * P : (u + 1) * P], ident[:])
-
-        def weave(k0, count, on_vector):
-            bank, col = turn_place(k0)
-            at = (k0 % 4) * 4 * P
-            dst = h_in[k0 // 4][:, at : at + count * 4 * P].bitcast(F32).rearrange("p (c s u) -> p c s u", c=count, u=2)
-            src = bank[:, col : col + count * 2 * P].rearrange("p (c u s) -> p c s u", c=count, u=2)
-            if on_vector:
-                nc.vector.tensor_copy(dst, src)
-            else:
+        def turn_and_weave(e):
+            bank = banks[(4, 5, 6, 7, 2)[e]]
+            for c in range(2):
+                words = h_rows[2 * e + c][:].bitcast(F32)
+                for u in range(2):
+                    col = (2 * c + u) * P
+                    nc.tensor.transpose(bank[:, col : col + P], words[:, u * P : (u + 1) * P], ident[:])
+            dst = h_place(HOT + e).bitcast(F32).rearrange("p (c s u) -> p c s u", c=2, u=2)
+            src = bank[:].rearrange("p (c u s) -> p c s u", c=2, u=2)
+            if e == COLD - 1:
                 nc.scalar.copy(dst, src)
+            else:
+                nc.vector.tensor_copy(dst, src)
 
-        def quantise(j):
+        def quantise(j, tag=None):
+            h_codes[j] = sb("h_codes%d" % j, [P, C * len(UNITS[j])], U32, tag=tag)
             nc.vector.quantize_mx(h_codes[j][:].bitcast(FP8X4), h_scales[j][:], h_in[j][:])
 
         chunk_words, chunk_scales = [], []
         word_piece = byte_piece = 0
         for k in range(S // P):
             if k == len(chunk_scales):
-                chunk_scales.extend(gather("gs", xs[:], U8, BYTE_PIECES, byte_piece, 2))
+                chunk_scales.extend(gather("gs", xs[:], U8, BYTE_PIECES, byte_piece))
                 byte_piece = byte_piece + 1
             if k == len(chunk_words):
-                chunk_words.extend(gather("gw", xw[:].bitcast(U32), U32, WORD_PIECES, word_piece, 3))
+                chunk_words.extend(gather("gw", xw[:].bitcast(U32), U32, WORD_PIECES, word_piece))
                 word_piece = word_piece + 1
             first_layer(k, chunk_words[k], chunk_scales[k])
-            e = k // 2
-            if k >= 16:
-                turn(k)
-            elif k % 2 == 1:
-                turn(k - 1)
-                turn(k)
-                if e in TURNS_ON_VECTOR:
-                    weave(k - 1, 2, True)
-                if e >= 2 and e - 2 not in TURNS_ON_VECTOR:
-                    weave(2 * (e - 2), 2, False)
-                for j in {3: (0,), 5: (1, 2), 7: (3,)}.get(e, ()):
-                    quantise(j)
-        weave(16, 1, False)
-        weave(17, 1, False)
+            if k in (1, 3, 5, 7):
+                turn_and_weave(k // 2)
+            if k == 7:
+                quantise(0, "h_rows7")
+                quantise(1)
+            if k == 13:
+                quantise(2)
+        turn_and_weave(COLD - 1)
+        quantise(3)
         quantise(4)
 
-        w2h_words_i = hot_words(w2h_words, 0, HOT)
-        w2c_words_i = w2c_words[:, 0].rearrange("e p b -> p e b").bitcast(I32)
-        w2h = [sb("w2h_first", [P, HOT, P], I32), sb("w2h_rest", [P, HOT, N - P], I32, tag="w1h_0")]
-        w2c = [sb("w2c_first", [P, COLD, P // 2], I32), sb("w2c_rest", [P, COLD, (N - P) // 2], I32, tag="w1h_1")]
-        nc.sync.dma_start(w2h[0][:], w2h_words_i[:, :, 0:P])
-        nc.sync.dma_start(w2c[0][:], w2c_words_i[:, :, 0 : P // 2])
+        w2h.append(sb("w2h_rest", [P, HOT, N - P], I32, tag="gw0"))
+        w2c.append(sb("w2c_rest", [P, COLD, (N - P) // 2], I32, tag="gw1"))
         gate_sb = sb("gate_sb", [P, TOP, T], F32, tag="warm_in")
         nc.sync.dma_start(gate_sb[:], gate.rearrange("r p t -> p r t"))
-        nc.sync.dma_start(w2h[1][:], w2h_words_i[:, :, P:N])
         nc.sync.dma_start(w2c[1][:], w2c_words_i[:, :, P // 2 : N // 2])
+        nc.sync.dma_start(w2h[1][:], w2h_words_i[:, :, P:N])
 
         y = [sb("y%d" % b, [P, S], F32) for b in range(4)]
+        ybanks = [banks[j] for j in (3, 0, 1, 2, 4)]
         for u in range(20):
             b, pair = divmod(u, 5)
-            bank = banks[(3, 4, 0, 1, 2)[u]] if b == 0 else banks[(5, 0, 4, 3, 6)[pair] if b == 1 else (1, 2, 5, 0)[(u - 10) % 4]]
+            bank = ybanks[pair]
             at = max(b - 1, 0) * P
-            experts = range(2 * pair, min(2 * pair + 2, E))
-            for e in experts:
+            experts = UNITS[pair]
+            for j, e in enumerate(experts):
                 if e < HOT:
                     w, ws = w2h[min(b, 1)][:, e, at : at + P].bitcast(FP8X4), s2h[4 * e : P, b * P : (b + 1) * P]
                 else:
                     w, ws = w2c[min(b, 1)][:, e - HOT, at // 2 : (at + P) // 2].bitcast(U8).bitcast(FP4X4), s2c[:, e - HOT, b * P : (b + 1) * P]
-                half = slice((e % 2) * C, (e % 2 + 1) * C)
+                half = slice(j * C, (j + 1) * C)
                 nc.tensor.matmul_mx(bank[:, half], lhsT=w, lhsT_scale=ws, rhs=h_codes[pair][:, half].bitcast(FP8X4),
                                     rhs_scale=h_scales[pair][:, half], start=True, stop=True)
             width = len(experts) * C
-            dst = y[b][:, 2 * pair * C : 2 * pair * C + width]
+            dst = y[b][:, experts[0] * C : experts[0] * C + width]
             if u in Y_ON_VECTOR:
                 nc.vector.tensor_copy(dst, bank[:, 0:width])
             else:
                 nc.scalar.copy(dst, bank[:, 0:width])
 
-        back_bank = [3, 6, 1, 2, 5]
+        back_bank = [5, 6, 7, 2, 5]
         first = [sb("first%d" % r, [P, 5 * P], F32) for r in range(TOP)]
         ring = [sb("ring%d" % r, [P, 5 * P], F32) for r in range(TOP)]
         out_rows = out_0.rearrange("(p t) k -> p t k", t=4)
@@ -220,7 +231,7 @@ def tile_moe_hot_mlp_silu_kernel(
                                      is_transpose=True, start=(r == 0), stop=(r == TOP - 1))
 
         def pair_bank(c0, half):
-            return banks[7] if half == 1 else banks[back_bank[c0 // 2]]
+            return ybanks[4] if half == 1 else ybanks[c0 // 2]
 
         def pair_places(c0, b):
             return [pair_bank(c0, b // 2)[:, (2 * j + b % 2) * P : (2 * j + b % 2 + 1) * P] for j in range(2)]
@@ -248,38 +259,38 @@ def tile_moe_hot_mlp_silu_kernel(
                            bank[:, 0 : 2 * P].rearrange("k (a p t) -> k a t p", p=4, t=4))
 
         for b, tiles in enumerate((first, ring)):
-            combine(tiles, 0, b, 0, 5, pair_places(0, b) + pair_places(2, b) + [banks[4][:, b * P : (b + 1) * P]])
+            combine(tiles, 0, b, 0, 5, pair_places(0, b) + pair_places(2, b) + [ybanks[2][:, b * P : (b + 1) * P]])
         sort_pair(0, 0)
         sort_pair(2, 0)
-        sort_single(banks[4], 0)
-        for tiles, col, b, c0 in ((first, 0, 2, 0), (first, 2 * P, 3, 0), (ring, 3 * P, 3, 2), (first, P, 2, 2)):
+        sort_single(ybanks[2], 0)
+        for tiles, col, b, c0 in ((first, 0, 2, 0), (first, 2 * P, 3, 0), (ring, 0, 2, 2), (ring, 2 * P, 3, 2)):
             combine(tiles, col, b, c0, 2, pair_places(c0, b))
-            if (b, c0) in ((3, 0), (2, 2)):
+            if b == 3:
                 sort_pair(c0, 1)
                 turn_back(c0)
                 turn_back(c0 + 1)
-        for b, tiles in ((2, first), (3, ring)):
-            combine(tiles, 3 * P, b, 4, 1, [banks[7][:, (b % 2) * P : (b % 2 + 1) * P]])
-        sort_single(banks[7], 1)
+        for b in (2, 3):
+            combine(first, (b % 2) * 2 * P, b, 4, 1, [ybanks[4][:, (b % 2) * P : (b % 2 + 1) * P]])
+        sort_single(ybanks[4], 1)
         turn_back(4)
 
         last = T // P - 1
         cols = slice(last * P, T)
-        half_bank = [banks[back_bank[2]], banks[7]]
+        half_bank = [banks[back_bank[2]], ybanks[4]]
         pairs = sb("pairs", [P, 2, P, 2], BF16)
         plain = sb("plain", [P, 4 * P], F32)
         for half in range(2):
             for b in (2 * half, 2 * half + 1):
-                combine(first if b else ring, (b or 4) * P, b, last, 1, [half_bank[half][:, (b % 2) * P : (b % 2 + 1) * P]])
+                combine(first if half else ring, (b % 2) * 2 * P, b, last, 1, [half_bank[half][:, (b % 2) * P : (b % 2 + 1) * P]])
             src = half_bank[half][:, 0 : 2 * P]
             nc.scalar.copy(pairs[:, :, half * 64 : half * 64 + 64, :], src.rearrange("k (p u e) -> k u p e", u=2, e=2))
             nc.scalar.copy(plain[:, half * 2 * P : (half + 1) * 2 * P], src)
         pair_words = pairs[:].rearrange("k u p e -> k (u p e)").bitcast(F32)
         for u in range(2):
-            nc.tensor.transpose(banks[3][:, u * P : (u + 1) * P], pair_words[:, u * P : (u + 1) * P], ident[:])
+            nc.tensor.transpose(ybanks[0][:, u * P : (u + 1) * P], pair_words[:, u * P : (u + 1) * P], ident[:])
         last_result = sb("last_result", [P, 4, P], F32)
         for half in range(2):
-            bank = banks[(6, 0)[half]]
+            bank = ybanks[1 + half]
             for j in range(2):
                 b = 2 * half + j
                 nc.tensor.transpose(bank[:, j * P : (j + 1) * P], plain[:, b * P : (b + 1) * P], ident[:])
@@ -305,7 +316,7 @@ def tile_moe_hot_mlp_silu_kernel(
         quantise_out(1, 0, 3 * P, 2 * P)
         nc.sync.dma_start(out_words[:, 0 : last * P], out_codes[:, 0 : last * P])
         nc.vector.tensor_copy(rounded[2][:].rearrange("p k t -> p (k t)").bitcast(F32).rearrange("p (k u) -> p k u", u=2),
-                              banks[3][:, 0 : 2 * P].rearrange("p (u k) -> p k u", u=2))
+                              ybanks[0][:, 0 : 2 * P].rearrange("p (u k) -> p k u", u=2))
         quantise_out(2, 0, last * P, P)
         nc.scalar.dma_start(out_words[:, cols], out_codes[:, cols])
         for r in range(4):

@@ -21,10 +21,12 @@ FP4X4 = mybir.dt.float4_e2m1fn_x4
 SILU = mybir.ActivationFunctionType.Silu
 MULT = mybir.AluOpType.mult
 
-WORD_PIECES = [(128, None), (128, None), (256, None), (256, None), (512, "gs0"), (512, "gs1"), (512, "gw3")]
-BYTE_PIECES = [(256, None), (256, None), (256, "gw0"), (512, "gw1"), (512, "gw2"), (512, "w1c_a")]
-UNITS = ((4, 5), (6, 7), (0, 1), (2, 3), (8,))
-Y_ON_VECTOR = (3, 4)
+WORD_PIECES = [(128, None), (128, None), (256, None), (512, None), (512, "gs0"), (512, "gs1"), (256, "gw3")]
+BYTE_PIECES = [(256, None), (256, None), (512, "gw0"), (512, "gw1"), (512, "gw2"), (256, "w1c_a")]
+ORDER = (4, 5, 0, 1, 2, 3, 6, 7, 8)
+TURNED = 2
+UNITS = ((0, 1), (2, 3), (4, 5), (6, 7), (8,))
+Y_ON_VECTOR = (2, 3)
 
 
 def tile_moe_hot_mlp_silu_kernel(
@@ -49,6 +51,8 @@ def tile_moe_hot_mlp_silu_kernel(
         w1c_a = sb("w1c_a", [P, 2, 2 * H], U8)
         w1c_b = sb("w1c_b", [P, 3, 2 * H], U8)
         w1_dealt = [sb("w1_dealt%d" % e, [P, H], I32) for e in range(HOT)]
+        w1c_dealt = [sb("w1c_dealt%d" % c, [P, 2 * H], U8) for c in range(COLD - TURNED)]
+        s1c_dealt = [sb("s1c_dealt%d" % c, [P, H], U8) for c in range(COLD - TURNED)]
         s1_dealt = sb("s1_dealt", [P, H], U8)
         s1h = sb("s1h", [P, H], U8)
         s2h = sb("s2h", [P, N], U8)
@@ -84,32 +88,44 @@ def tile_moe_hot_mlp_silu_kernel(
         nc.sync.dma_start(xw[:], x_words[0].rearrange("p t d -> p (t d)").bitcast(I32))
         nc.sync.dma_start(w1c_a[:].bitcast(I32), w1c_words[0:2, 0].rearrange("e p b -> p e b").bitcast(I32))
         load_cold_scales(s1c, w1c_scales)
-        nc.sync.dma_start(w1c_b[:].bitcast(I32), w1c_words[2:COLD, 0].rearrange("e p b -> p e b").bitcast(I32))
         load_hot_scales(s1h, w1h_scales)
         for j in range(2):
             nc.sync.dma_start(w1h[j][:], hot_words(w1h_words, 2 * j, 2 * j + 2))
+        nc.sync.dma_start(w1c_b[:].bitcast(I32), w1c_words[2:COLD, 0].rearrange("e p b -> p e b").bitcast(I32))
 
-        def deal(dst, src):
-            nc.gpsimd.tensor_copy(dst.rearrange("p (t m) -> p t m", t=4), src.rearrange("p (m t) -> p t m", t=4))
+        def deal(dst, src, run):
+            nc.gpsimd.tensor_copy(dst.rearrange("p (t a i) -> p a t i", t=4, i=run), src.rearrange("p (a i t) -> p a t i", t=4, i=run))
 
-        deal(s1_dealt[:], s1h[:])
-        for e in range(HOT):
-            deal(w1_dealt[e][:], w1h[e // 2][:, e % 2, :])
+        for e in ORDER[TURNED:]:
+            if e == 0:
+                deal(s1_dealt[:], s1h[:], 16)
+            if e < HOT:
+                deal(w1_dealt[e][:], w1h[e // 2][:, e % 2, :], 4)
+            else:
+                c = e - HOT
+                deal(s1c_dealt[c - TURNED][:], s1c[:, c, :], 16)
+                deal(w1c_dealt[c - TURNED][:].bitcast(U16), w1c_b[:, c - 2, :].bitcast(U16), 8)
 
         w2h_words_i = hot_words(w2h_words, 0, HOT)
         w2c_words_i = w2c_words[:, 0].rearrange("e p b -> p e b").bitcast(I32)
         w2h = [sb("w2h_first", [P, HOT, P], I32)]
         w2c = [sb("w2c_first", [P, COLD, P // 2], I32)]
-        load_cold_scales(s2c, w2c_scales)
-        nc.sync.dma_start(w2c[0][:], w2c_words_i[:, :, 0 : P // 2])
         load_hot_scales(s2h, w2h_scales)
         nc.sync.dma_start(w2h[0][:], w2h_words_i[:, :, 0:P])
+        nc.sync.dma_start(w2c[0][:], w2c_words_i[:, :, 0 : P // 2])
+        load_cold_scales(s2c, w2c_scales)
+        w2h.append(sb("w2h_rest", [P, HOT, N - P], I32))
+        w2c.append(sb("w2c_rest", [P, COLD, (N - P) // 2], I32))
+        nc.sync.dma_start(w2h[1][:], w2h_words_i[:, :, P:N])
+        nc.sync.dma_start(w2c[1][:], w2c_words_i[:, :, P // 2 : N // 2])
+        gate_sb = sb("gate_sb", [P, TOP, T], F32, tag="warm_in")
+        nc.sync.dma_start(gate_sb[:], gate.rearrange("r p t -> p r t"))
         for r, pos in enumerate((pos1, pos2, pos3)):
             nc.sync.dma_start(pos_sb[r][:], pos)
 
         h_in = [sb("h_in%d" % j, [P, 4 * C * len(unit)], BF16) for j, unit in enumerate(UNITS)]
         h_scales = [sb("h_scales%d" % j, [P, C * len(unit)], U8) for j, unit in enumerate(UNITS)]
-        h_rows = [sb("h_rows%d" % k, [P, H], BF16) for k in range(2 * COLD)]
+        h_rows = [sb("h_rows%d" % k, [P, H], BF16) for k in range(2 * TURNED)]
         h_codes = {}
 
         def h_place(e):
@@ -118,18 +134,24 @@ def tile_moe_hot_mlp_silu_kernel(
             return h_in[j][:, at : at + 4 * C]
 
         def gather(name, window, dtype, pieces, j):
-            slot0, (n, tag) = (HOT * C + sum(piece[0] for piece in pieces[:j])) % S, pieces[j]
+            done, (n, tag) = sum(piece[0] for piece in pieces[:j]), pieces[j]
+            slot0 = ORDER[done // C] * C + done % C
             dst = sb("%s%d" % (name, j), [P, n], dtype, tag=tag)
             nc.vector.tensor_copy(dst[:], window.indirect(offs_sb[:, slot0 // 16 : (slot0 + n) // 16]))
             return [dst[:, c * P : (c + 1) * P] for c in range(n // P)]
 
         def first_layer(k, words, scales):
-            e = (k // 2 + HOT) % E
-            bank = banks[k % 4]
-            if e < HOT:
+            e = ORDER[k // 2]
+            bank = banks[k % 5]
+            if k >= 2 * TURNED:
                 for t in range(4):
                     cols = slice(t * P, (t + 1) * P)
-                    nc.tensor.matmul_mx(bank[:, cols], lhsT=w1_dealt[e][:, cols].bitcast(FP8X4), lhsT_scale=s1_dealt[4 * e : P, cols],
+                    if e < HOT:
+                        w, ws = w1_dealt[e][:, cols].bitcast(FP8X4), s1_dealt[4 * e : P, cols]
+                    else:
+                        c = e - HOT - TURNED
+                        w, ws = w1c_dealt[c][:, 2 * t * P : 2 * (t + 1) * P].bitcast(FP4X4), s1c_dealt[c][:, cols]
+                    nc.tensor.matmul_mx(bank[:, cols], lhsT=w, lhsT_scale=ws,
                                         rhs=words.bitcast(FP8X4), rhs_scale=scales, start=True, stop=True)
                 at = (k % 2) * 4 * P
                 nc.scalar.activation(h_place(e)[:, at : at + 4 * P].rearrange("p (s t) -> p s t", t=4),
@@ -143,7 +165,7 @@ def tile_moe_hot_mlp_silu_kernel(
                                  bank[:].rearrange("s (p u e) -> s u p e", u=2, e=2), SILU)
 
         def turn_and_weave(e):
-            bank = banks[(4, 5, 6, 7, 2)[e]]
+            bank = banks[5 + e]
             for c in range(2):
                 words = h_rows[2 * e + c][:].bitcast(F32)
                 for u in range(2):
@@ -151,10 +173,7 @@ def tile_moe_hot_mlp_silu_kernel(
                     nc.tensor.transpose(bank[:, col : col + P], words[:, u * P : (u + 1) * P], ident[:])
             dst = h_place(HOT + e).bitcast(F32).rearrange("p (c s u) -> p c s u", c=2, u=2)
             src = bank[:].rearrange("p (c u s) -> p c s u", c=2, u=2)
-            if e == COLD - 1:
-                nc.scalar.copy(dst, src)
-            else:
-                nc.vector.tensor_copy(dst, src)
+            nc.vector.tensor_copy(dst, src)
 
         def quantise(j, tag=None):
             h_codes[j] = sb("h_codes%d" % j, [P, C * len(UNITS[j])], U32, tag=tag)
@@ -170,29 +189,21 @@ def tile_moe_hot_mlp_silu_kernel(
                 chunk_words.extend(gather("gw", xw[:].bitcast(U32), U32, WORD_PIECES, word_piece))
                 word_piece = word_piece + 1
             first_layer(k, chunk_words[k], chunk_scales[k])
-            if k in (1, 3, 5, 7):
+            if k % 2 == 1 and k < 2 * TURNED:
                 turn_and_weave(k // 2)
-            if k == 7:
-                quantise(0, "h_rows7")
-                quantise(1)
             if k == 13:
-                quantise(2)
-        turn_and_weave(COLD - 1)
-        quantise(3)
-        quantise(4)
+                quantise(0)
+                quantise(2, "w1c_dealt0")
+        for j in (1, 3, 4):
+            quantise(j)
 
-        w2h.append(sb("w2h_rest", [P, HOT, N - P], I32, tag="gw0"))
-        w2c.append(sb("w2c_rest", [P, COLD, (N - P) // 2], I32, tag="gw1"))
-        gate_sb = sb("gate_sb", [P, TOP, T], F32, tag="warm_in")
-        nc.sync.dma_start(gate_sb[:], gate.rearrange("r p t -> p r t"))
-        nc.sync.dma_start(w2c[1][:], w2c_words_i[:, :, P // 2 : N // 2])
-        nc.sync.dma_start(w2h[1][:], w2h_words_i[:, :, P:N])
 
         y = [sb("y%d" % b, [P, S], F32) for b in range(4)]
-        ybanks = [banks[j] for j in (3, 0, 1, 2, 4)]
+        first_banks = [banks[j] for j in (3, 4, 1, 2, 0)]
+        ybanks = [first_banks[j] for j in (1, 3, 4, 0, 2)]
         for u in range(20):
             b, pair = divmod(u, 5)
-            bank = ybanks[pair]
+            bank = first_banks[pair] if b == 0 else ybanks[4] if pair == 4 else ybanks[(4 * b + pair - 4) % 3]
             at = max(b - 1, 0) * P
             experts = UNITS[pair]
             for j, e in enumerate(experts):
@@ -210,7 +221,9 @@ def tile_moe_hot_mlp_silu_kernel(
             else:
                 nc.scalar.copy(dst, bank[:, 0:width])
 
-        back_bank = [5, 6, 7, 2, 5]
+
+        back_banks = [banks[5], banks[6], banks[7], ybanks[0], ybanks[1]]
+        late_banks = [ybanks[4], ybanks[3]]
         first = [sb("first%d" % r, [P, 5 * P], F32) for r in range(TOP)]
         ring = [sb("ring%d" % r, [P, 5 * P], F32) for r in range(TOP)]
         out_rows = out_0.rearrange("(p t) k -> p t k", t=4)
@@ -219,34 +232,39 @@ def tile_moe_hot_mlp_silu_kernel(
         rounded = [sb("rounded0", [P, 3 * P, 4], BF16)]
         results = []
 
-        def combine(tiles, col, b, c0, count, targets):
+        def combine(tiles, col, b, c0, count, targets, apart=False):
             for r in range(TOP):
                 product = tiles[r][:, col : col + count * P]
                 t0 = c0 * P
                 nc.vector.tensor_tensor(product, y[b][:].indirect(pos_sb[r][:, t0 // 16 : (t0 + count * P) // 16]),
                                         gate_sb[:, r, t0 : t0 + count * P], MULT)
-            for j in range(count):
-                for r in range(TOP):
-                    nc.tensor.matmul(targets[j], lhsT=tiles[r][:, col + j * P : col + (j + 1) * P], rhs=ident[:],
-                                     is_transpose=True, start=(r == 0), stop=(r == TOP - 1))
-
-        def pair_bank(c0, half):
-            return ybanks[4] if half == 1 else ybanks[c0 // 2]
+            steps = [(j, r) for r in range(TOP) for j in range(count)] if apart else [(j, r) for j in range(count) for r in range(TOP)]
+            for j, r in steps:
+                nc.tensor.matmul(targets[j], lhsT=tiles[r][:, col + j * P : col + (j + 1) * P], rhs=ident[:],
+                                 is_transpose=True, start=(r == 0), stop=(r == TOP - 1))
 
         def pair_places(c0, b):
-            return [pair_bank(c0, b // 2)[:, (2 * j + b % 2) * P : (2 * j + b % 2 + 1) * P] for j in range(2)]
+            return [ybanks[c0 // 2][:, (2 * j + b) * P : (2 * j + b + 1) * P] for j in range(2)]
+
+        def late_place(c, b):
+            return late_banks[c % 2][:, (b % 2) * P : (b % 2 + 1) * P]
 
         sums = [sb("sums%d" % g, [P, n, 4, P], F32) for g, n in enumerate((2, 2, 1))]
 
-        def sort_pair(c0, half):
-            nc.scalar.copy(sums[c0 // 2][:, :, :, 64 * half : 64 * half + 64].rearrange("k c t (a p) -> k c a t p", p=4),
-                           pair_bank(c0, half)[:].rearrange("k (c a p t) -> k c a t p", c=2, p=4, t=4))
+        def sort_pair(c0):
+            nc.scalar.copy(sums[c0 // 2][:, :, :, 0:64].rearrange("k c t (a p) -> k c a t p", p=4),
+                           ybanks[c0 // 2][:].rearrange("k (c a p t) -> k c a t p", c=2, p=4, t=4))
+
+        def sort_single(c, bank, half):
+            nc.scalar.copy(sums[c // 2][:, c % 2, :, 64 * half : 64 * half + 64].rearrange("k t (a p) -> k a t p", p=4),
+                           bank[:, 0 : 2 * P].rearrange("k (a p t) -> k a t p", p=4, t=4))
 
         def turn_back(c):
-            bank = banks[back_bank[c]]
             for t in range(4):
-                nc.tensor.transpose(bank[:, t * P : (t + 1) * P], sums[c // 2][:, c % 2, t, :], ident[:])
-            view = bank[:].rearrange("p (t k) -> p t k", t=4)
+                nc.tensor.transpose(back_banks[c][:, t * P : (t + 1) * P], sums[c // 2][:, c % 2, t, :], ident[:])
+
+        def finish(c):
+            view = back_banks[c][:].rearrange("p (t k) -> p t k", t=4)
             result = sb("result%d" % c, [P, 4, P], F32)
             nc.scalar.copy(result[:], view)
             results.append(result)
@@ -254,29 +272,31 @@ def tile_moe_hot_mlp_silu_kernel(
                 nc.scalar.copy(rounded[0][:, c * P : (c + 1) * P, :], view.rearrange("p t k -> p k t"))
             nc.sync.dma_start(out_rows[:, :, c * P : (c + 1) * P], result[:])
 
-        def sort_single(bank, half):
-            nc.scalar.copy(sums[2][:, 0, :, 64 * half : 64 * half + 64].rearrange("k t (a p) -> k a t p", p=4),
-                           bank[:, 0 : 2 * P].rearrange("k (a p t) -> k a t p", p=4, t=4))
-
         for b, tiles in enumerate((first, ring)):
             combine(tiles, 0, b, 0, 5, pair_places(0, b) + pair_places(2, b) + [ybanks[2][:, b * P : (b + 1) * P]])
-        sort_pair(0, 0)
-        sort_pair(2, 0)
-        sort_single(ybanks[2], 0)
-        for tiles, col, b, c0 in ((first, 0, 2, 0), (first, 2 * P, 3, 0), (ring, 0, 2, 2), (ring, 2 * P, 3, 2)):
-            combine(tiles, col, b, c0, 2, pair_places(c0, b))
-            if b == 3:
-                sort_pair(c0, 1)
-                turn_back(c0)
-                turn_back(c0 + 1)
+        sort_pair(0)
+        sort_pair(2)
+        sort_single(4, ybanks[2], 0)
+        for tiles, c0 in ((first, 0), (ring, 2)):
+            for b in (2, 3):
+                combine(tiles, (b % 2) * 2 * P, b, c0, 2, [late_place(c0, b), late_place(c0 + 1, b)], apart=True)
+            for c in (c0, c0 + 1):
+                sort_single(c, late_banks[c % 2], 1)
+            turn_back(c0)
+            finish(c0)
+            turn_back(c0 + 1)
+            if c0 == 0:
+                finish(1)
         for b in (2, 3):
-            combine(first, (b % 2) * 2 * P, b, 4, 1, [ybanks[4][:, (b % 2) * P : (b % 2 + 1) * P]])
-        sort_single(ybanks[4], 1)
+            combine(first, (b % 2) * 2 * P, b, 4, 1, [late_place(4, b)])
+        sort_single(4, late_banks[0], 1)
+        finish(3)
         turn_back(4)
+        finish(4)
 
         last = T // P - 1
         cols = slice(last * P, T)
-        half_bank = [banks[back_bank[2]], ybanks[4]]
+        half_bank = [late_banks[0], back_banks[4]]
         pairs = sb("pairs", [P, 2, P, 2], BF16)
         plain = sb("plain", [P, 4 * P], F32)
         for half in range(2):
@@ -287,10 +307,10 @@ def tile_moe_hot_mlp_silu_kernel(
             nc.scalar.copy(plain[:, half * 2 * P : (half + 1) * 2 * P], src)
         pair_words = pairs[:].rearrange("k u p e -> k (u p e)").bitcast(F32)
         for u in range(2):
-            nc.tensor.transpose(ybanks[0][:, u * P : (u + 1) * P], pair_words[:, u * P : (u + 1) * P], ident[:])
+            nc.tensor.transpose(ybanks[2][:, u * P : (u + 1) * P], pair_words[:, u * P : (u + 1) * P], ident[:])
         last_result = sb("last_result", [P, 4, P], F32)
         for half in range(2):
-            bank = ybanks[1 + half]
+            bank = banks[5 + half]
             for j in range(2):
                 b = 2 * half + j
                 nc.tensor.transpose(bank[:, j * P : (j + 1) * P], plain[:, b * P : (b + 1) * P], ident[:])
@@ -316,7 +336,7 @@ def tile_moe_hot_mlp_silu_kernel(
         quantise_out(1, 0, 3 * P, 2 * P)
         nc.sync.dma_start(out_words[:, 0 : last * P], out_codes[:, 0 : last * P])
         nc.vector.tensor_copy(rounded[2][:].rearrange("p k t -> p (k t)").bitcast(F32).rearrange("p (k u) -> p k u", u=2),
-                              ybanks[0][:, 0 : 2 * P].rearrange("p (u k) -> p k u", u=2))
+                              ybanks[2][:, 0 : 2 * P].rearrange("p (u k) -> p k u", u=2))
         quantise_out(2, 0, last * P, P)
         nc.scalar.dma_start(out_words[:, cols], out_codes[:, cols])
         for r in range(4):

@@ -47,12 +47,11 @@ def tile_moe_hot_mlp_silu_kernel(
         pos_sb = [sb("pos_sb%d" % r, [P, T // 16], U16) for r in range(TOP)]
         xw = sb("xw", [P, T], I32)
         xs = sb("xs", [P, T], U8)
-        w1h = [sb("w1h_%d" % j, [P, 2, H], I32) for j in range(2)]
+        w1h = [sb("w1h_%d" % j, [P, n, H], I32) for j, n in enumerate((1, 1, 2))]
         w1c_a = sb("w1c_a", [P, 2, 2 * H], U8)
         w1c_b = sb("w1c_b", [P, 3, 2 * H], U8)
         w1_dealt = [sb("w1_dealt%d" % e, [P, H], I32) for e in range(HOT)]
         w1c_dealt = [sb("w1c_dealt%d" % c, [P, 2 * H], U8) for c in range(COLD - TURNED)]
-        s1c_dealt = [sb("s1c_dealt%d" % c, [P, H], U8) for c in range(COLD - TURNED)]
         s1_dealt = sb("s1_dealt", [P, H], U8)
         s1h = sb("s1h", [P, H], U8)
         s2h = sb("s2h", [P, N], U8)
@@ -88,23 +87,27 @@ def tile_moe_hot_mlp_silu_kernel(
         nc.sync.dma_start(xw[:], x_words[0].rearrange("p t d -> p (t d)").bitcast(I32))
         nc.sync.dma_start(w1c_a[:].bitcast(I32), w1c_words[0:2, 0].rearrange("e p b -> p e b").bitcast(I32))
         load_cold_scales(s1c, w1c_scales)
+        nc.sync.dma_start(w1h[0][:], hot_words(w1h_words, 0, 1))
         load_hot_scales(s1h, w1h_scales)
-        for j in range(2):
-            nc.sync.dma_start(w1h[j][:], hot_words(w1h_words, 2 * j, 2 * j + 2))
+        nc.sync.dma_start(w1h[1][:], hot_words(w1h_words, 1, 2))
+        nc.sync.dma_start(w1h[2][:], hot_words(w1h_words, 2, HOT))
         nc.sync.dma_start(w1c_b[:].bitcast(I32), w1c_words[2:COLD, 0].rearrange("e p b -> p e b").bitcast(I32))
 
         def deal(dst, src, run):
             nc.gpsimd.tensor_copy(dst.rearrange("p (t a i) -> p a t i", t=4, i=run), src.rearrange("p (a i t) -> p a t i", t=4, i=run))
 
-        for e in ORDER[TURNED:]:
-            if e == 0:
-                deal(s1_dealt[:], s1h[:], 16)
-            if e < HOT:
-                deal(w1_dealt[e][:], w1h[e // 2][:, e % 2, :], 4)
-            else:
-                c = e - HOT
-                deal(s1c_dealt[c - TURNED][:], s1c[:, c, :], 16)
-                deal(w1c_dealt[c - TURNED][:].bitcast(U16), w1c_b[:, c - 2, :].bitcast(U16), 8)
+        def deal_cold(c):
+            deal(s1c_dealt[c], s1c[:, TURNED + c, :], 16)
+            deal(w1c_dealt[c][:].bitcast(U16), w1c_b[:, c, :].bitcast(U16), 8)
+
+        deal(s1_dealt[:], s1h[:], 16)
+        for e in range(HOT):
+            deal(w1_dealt[e][:], w1h[min(e, 2)][:, max(e - 2, 0), :], 4)
+        early_plane = sb("early_plane", [P, H], U8)
+        late_planes = sb("late_planes", [P, 2, H], U8, tag="w1h_2")
+        s1c_dealt = [early_plane[:], late_planes[:, 0, :], late_planes[:, 1, :]]
+        for c in range(COLD - TURNED):
+            deal_cold(c)
 
         w2h_words_i = hot_words(w2h_words, 0, HOT)
         w2c_words_i = w2c_words[:, 0].rearrange("e p b -> p e b").bitcast(I32)

@@ -24,9 +24,9 @@ MULT = mybir.AluOpType.mult
 WORD_PIECES = [(128, None), (128, None), (256, None), (512, None), (512, "gs0"), (512, "gs1"), (256, "gw3")]
 BYTE_PIECES = [(256, None), (256, None), (512, "gw0"), (512, "gw1"), (512, "gw2"), (256, "w1c_a")]
 ORDER = (4, 5, 0, 1, 2, 3, 6, 7, 8)
-TURNED = 2
+TURNED = 1
 UNITS = ((0, 1), (2, 3), (4, 5), (6, 7), (8,))
-Y_ON_VECTOR = (2, 3)
+Y_ON_VECTOR = (0, 3)
 
 
 def tile_moe_hot_mlp_silu_kernel(
@@ -98,15 +98,17 @@ def tile_moe_hot_mlp_silu_kernel(
 
         def deal_cold(c):
             deal(s1c_dealt[c], s1c[:, TURNED + c, :], 16)
-            deal(w1c_dealt[c][:].bitcast(U16), w1c_b[:, c, :].bitcast(U16), 8)
+            words = w1c_b[:, c - 1, :] if c else w1c_a[:, 1, :]
+            deal(w1c_dealt[c][:].bitcast(U16), words.bitcast(U16), 8)
 
+        early_plane = sb("early_plane", [P, H], U8)
+        late_planes = sb("late_planes", [P, 3, H], U8, tag="w1h_2")
+        s1c_dealt = [early_plane[:]] + [late_planes[:, j, :] for j in range(3)]
+        deal_cold(0)
         deal(s1_dealt[:], s1h[:], 16)
         for e in range(HOT):
             deal(w1_dealt[e][:], w1h[min(e, 2)][:, max(e - 2, 0), :], 4)
-        early_plane = sb("early_plane", [P, H], U8)
-        late_planes = sb("late_planes", [P, 2, H], U8, tag="w1h_2")
-        s1c_dealt = [early_plane[:], late_planes[:, 0, :], late_planes[:, 1, :]]
-        for c in range(COLD - TURNED):
+        for c in range(1, COLD - TURNED):
             deal_cold(c)
 
         w2h_words_i = hot_words(w2h_words, 0, HOT)
@@ -196,14 +198,14 @@ def tile_moe_hot_mlp_silu_kernel(
                 turn_and_weave(k // 2)
             if k == 13:
                 quantise(0)
-                quantise(2, "w1c_dealt0")
+                quantise(2, "w1c_dealt1")
         for j in (1, 3, 4):
             quantise(j)
 
 
         y = [sb("y%d" % b, [P, S], F32) for b in range(4)]
-        first_banks = [banks[j] for j in (3, 4, 1, 2, 0)]
-        ybanks = [first_banks[j] for j in (1, 3, 4, 0, 2)]
+        first_banks = [banks[j] for j in (6, 3, 4, 2, 0)]
+        ybanks = [banks[j] for j in (4, 2, 0, 3, 1)]
         for u in range(20):
             b, pair = divmod(u, 5)
             bank = first_banks[pair] if b == 0 else ybanks[4] if pair == 4 else ybanks[(4 * b + pair - 4) % 3]
@@ -331,13 +333,14 @@ def tile_moe_hot_mlp_silu_kernel(
             nc.vector.quantize_mx(out_codes[:, t0 : t0 + n].bitcast(FP8X4), out_scales[:, t0 : t0 + n],
                                   rounded[g][:, at : at + n, :].rearrange("p k t -> p (k t)"))
 
+        quantise_out(0, 0, 0, 2 * P)
+        nc.sync.dma_start(out_words[:, 0 : 2 * P], out_codes[:, 0 : 2 * P])
         for c in (3, 4):
             nc.vector.tensor_copy(rounded[1][:, (c - 3) * P : (c - 2) * P, :].rearrange("p (a k) t -> p a t k", k=4),
                                   results[c][:].rearrange("p t (a k) -> p a t k", k=4))
-        quantise_out(0, 0, 0, 2 * P)
         quantise_out(0, 2 * P, 2 * P, P)
         quantise_out(1, 0, 3 * P, 2 * P)
-        nc.sync.dma_start(out_words[:, 0 : last * P], out_codes[:, 0 : last * P])
+        nc.sync.dma_start(out_words[:, 2 * P : last * P], out_codes[:, 2 * P : last * P])
         nc.vector.tensor_copy(rounded[2][:].rearrange("p k t -> p (k t)").bitcast(F32).rearrange("p (k u) -> p k u", u=2),
                               ybanks[2][:, 0 : 2 * P].rearrange("p (u k) -> p k u", u=2))
         quantise_out(2, 0, last * P, P)

@@ -19,6 +19,7 @@ U8 = mybir.dt.uint8
 FP8X4 = mybir.dt.float8_e4m3fn_x4
 FP4X4 = mybir.dt.float4_e2m1fn_x4
 SILU = mybir.ActivationFunctionType.Silu
+COPY = mybir.ActivationFunctionType.Copy
 MULT = mybir.AluOpType.mult
 
 WORD_PIECES = [(128, None), (128, None), (256, None), (512, None), (512, "gs0"), (512, "gs1"), (256, "gw3")]
@@ -123,10 +124,13 @@ def tile_moe_hot_mlp_silu_kernel(
         w2c.append(sb("w2c_rest", [P, COLD, (N - P) // 2], I32))
         nc.sync.dma_start(w2h[1][:], w2h_words_i[:, :, P:N])
         nc.sync.dma_start(w2c[1][:], w2c_words_i[:, :, P // 2 : N // 2])
-        gate_sb = sb("gate_sb", [P, TOP, T], F32, tag="warm_in")
-        nc.sync.dma_start(gate_sb[:], gate.rearrange("r p t -> p r t"))
+        gate_sb = sb("gate_sb", [P, TOP, T - P], F32, tag="warm_in")
+        nc.sync.dma_start(gate_sb[:], gate[:, :, P:T].rearrange("r p t -> p r t"))
         for r, pos in enumerate((pos1, pos2, pos3)):
             nc.sync.dma_start(pos_sb[r][:], pos)
+        own_gate = sb("own_gate", [P, TOP], F32)
+        with nc.allow_non_contiguous_dma(reason="one weight a partition"):
+            nc.sync.dma_start(own_gate[:], gate[:, 0, 0:P].rearrange("r p -> p r"))
 
         h_in = [sb("h_in%d" % j, [P, 4 * C * len(unit)], BF16) for j, unit in enumerate(UNITS)]
         h_scales = [sb("h_scales%d" % j, [P, C * len(unit)], U8) for j, unit in enumerate(UNITS)]
@@ -204,11 +208,10 @@ def tile_moe_hot_mlp_silu_kernel(
 
 
         y = [sb("y%d" % b, [P, S], F32) for b in range(4)]
-        first_banks = [banks[j] for j in (6, 3, 4, 2, 0)]
-        ybanks = [banks[j] for j in (4, 2, 0, 3, 1)]
+        y_banks = ((6, 3, 4, 2, 0), (4, 2, 0, 1, 4), (2, 0, 1, 4, 2), (0, 4, 2, 0, 4))
         for u in range(20):
             b, pair = divmod(u, 5)
-            bank = first_banks[pair] if b == 0 else ybanks[4] if pair == 4 else ybanks[(4 * b + pair - 4) % 3]
+            bank = banks[y_banks[b][pair]]
             at = max(b - 1, 0) * P
             experts = UNITS[pair]
             for j, e in enumerate(experts):
@@ -226,125 +229,82 @@ def tile_moe_hot_mlp_silu_kernel(
             else:
                 nc.scalar.copy(dst, bank[:, 0:width])
 
-
-        back_banks = [banks[5], banks[6], banks[7], ybanks[0], ybanks[1]]
-        late_banks = [ybanks[4], ybanks[3]]
         first = [sb("first%d" % r, [P, 5 * P], F32) for r in range(TOP)]
         ring = [sb("ring%d" % r, [P, 5 * P], F32) for r in range(TOP)]
+        own = [sb("own%d" % r, [P, 4 * P], F32) for r in range(TOP)]
+        own_sums = [sb("own_sums%d" % r, [P, 4, P], F32) for r in range(TOP)]
+        sums = sb("sums", [P, 4, 4, P], F32)
+        last_sums = sb("last_sums", [P, 1, 4, P], F32)
         out_rows = out_0.rearrange("(p t) k -> p t k", t=4)
-        out_blocks = out_0.rearrange("(b p) k -> p b k", p=P)
         out_words = out_1[0].rearrange("p t d -> p (t d)").bitcast(I32)
-        rounded = [sb("rounded0", [P, 3 * P, 4], BF16)]
-        results = []
+        results = {}
 
-        def combine(tiles, col, b, c0, count, targets, apart=False):
+        def combine(tiles, col, b, c0, targets):
+            count = len(targets)
             for r in range(TOP):
-                product = tiles[r][:, col : col + count * P]
                 t0 = c0 * P
-                nc.vector.tensor_tensor(product, y[b][:].indirect(pos_sb[r][:, t0 // 16 : (t0 + count * P) // 16]),
-                                        gate_sb[:, r, t0 : t0 + count * P], MULT)
-            steps = [(j, r) for r in range(TOP) for j in range(count)] if apart else [(j, r) for j in range(count) for r in range(TOP)]
-            for j, r in steps:
-                nc.tensor.matmul(targets[j], lhsT=tiles[r][:, col + j * P : col + (j + 1) * P], rhs=ident[:],
-                                 is_transpose=True, start=(r == 0), stop=(r == TOP - 1))
+                nc.vector.tensor_tensor(tiles[r][:, col : col + count * P],
+                                        y[b][:].indirect(pos_sb[r][:, t0 // 16 : (t0 + count * P) // 16]),
+                                        gate_sb[:, r, t0 - P : t0 - P + count * P], MULT)
+            for j in range(count):
+                for r in range(TOP):
+                    nc.tensor.matmul(targets[j], lhsT=tiles[r][:, col + j * P : col + (j + 1) * P], rhs=ident[:],
+                                     is_transpose=True, start=(r == 0), stop=(r == TOP - 1))
 
-        def pair_places(c0, b):
-            return [ybanks[c0 // 2][:, (2 * j + b) * P : (2 * j + b + 1) * P] for j in range(2)]
+        def quarter(bank, j):
+            return banks[bank][:, j * P : (j + 1) * P]
 
-        def late_place(c, b):
-            return late_banks[c % 2][:, (b % 2) * P : (b % 2 + 1) * P]
+        def sort(dst, bank, chunks, b0, blocks):
+            nc.scalar.copy(dst[:, :, :, 32 * b0 : 32 * (b0 + blocks)].rearrange("k c t (a p) -> k c a t p", p=4),
+                           banks[bank][:, 0 : chunks * blocks * P].rearrange("k (c a p t) -> k c a t p", c=chunks, p=4, t=4))
 
-        sums = [sb("sums%d" % g, [P, n, 4, P], F32) for g, n in enumerate((2, 2, 1))]
-
-        def sort_pair(c0):
-            nc.scalar.copy(sums[c0 // 2][:, :, :, 0:64].rearrange("k c t (a p) -> k c a t p", p=4),
-                           ybanks[c0 // 2][:].rearrange("k (c a p t) -> k c a t p", c=2, p=4, t=4))
-
-        def sort_single(c, bank, half):
-            nc.scalar.copy(sums[c // 2][:, c % 2, :, 64 * half : 64 * half + 64].rearrange("k t (a p) -> k a t p", p=4),
-                           bank[:, 0 : 2 * P].rearrange("k (a p t) -> k a t p", p=4, t=4))
-
-        def turn_back(c):
+        def finish(c, bank, parts):
             for t in range(4):
-                nc.tensor.transpose(back_banks[c][:, t * P : (t + 1) * P], sums[c // 2][:, c % 2, t, :], ident[:])
+                for j, part in enumerate(parts):
+                    nc.tensor.matmul(quarter(bank, t), lhsT=part[:, t, :], rhs=ident[:],
+                                     is_transpose=True, start=(j == 0), stop=(j == len(parts) - 1))
+            results[c] = sb("result%d" % c, [P, 4, P], F32)
+            nc.scalar.copy(results[c][:], banks[bank][:].rearrange("p (t k) -> p t k", t=4))
+            nc.sync.dma_start(out_rows[:, :, c * P : (c + 1) * P], results[c][:])
 
-        def finish(c):
-            view = back_banks[c][:].rearrange("p (t k) -> p t k", t=4)
-            result = sb("result%d" % c, [P, 4, P], F32)
-            nc.scalar.copy(result[:], view)
-            results.append(result)
-            if c < 3:
-                nc.scalar.copy(rounded[0][:, c * P : (c + 1) * P, :], view.rearrange("p t k -> p k t"))
-            nc.sync.dma_start(out_rows[:, :, c * P : (c + 1) * P], result[:])
-
-        for b, tiles in enumerate((first, ring)):
-            combine(tiles, 0, b, 0, 5, pair_places(0, b) + pair_places(2, b) + [ybanks[2][:, b * P : (b + 1) * P]])
-        sort_pair(0)
-        sort_pair(2)
-        sort_single(4, ybanks[2], 0)
-        for tiles, c0 in ((first, 0), (ring, 2)):
-            for b in (2, 3):
-                combine(tiles, (b % 2) * 2 * P, b, c0, 2, [late_place(c0, b), late_place(c0 + 1, b)], apart=True)
-            for c in (c0, c0 + 1):
-                sort_single(c, late_banks[c % 2], 1)
-            turn_back(c0)
-            finish(c0)
-            turn_back(c0 + 1)
-            if c0 == 0:
-                finish(1)
+        combine(first, 0, 0, 1, [quarter(1, j) for j in range(4)] + [quarter(4, 0)])
+        combine(ring, 0, 1, 1, [quarter(2, j) for j in range(4)] + [quarter(4, 1)])
+        for b in range(4):
+            for r in range(TOP):
+                nc.scalar.activation(own[r][:, b * P : (b + 1) * P], y[b][:].indirect(pos_sb[r][:, 0 : P // 16]), COPY)
+                nc.tensor.transpose(quarter(5 + r, b), own[r][:, b * P : (b + 1) * P], ident[:])
         for b in (2, 3):
-            combine(first, (b % 2) * 2 * P, b, 4, 1, [late_place(4, b)])
-        sort_single(4, late_banks[0], 1)
-        finish(3)
-        turn_back(4)
-        finish(4)
+            combine(first, (b - 2) * 2 * P, b, 1, [quarter(0, b - 2), quarter(0, b)])
+        sort(sums[:], 1, 4, 0, 1)
+        sort(sums[:], 2, 4, 1, 1)
+        sort(last_sums[:], 4, 1, 0, 2)
+        for r in range(TOP):
+            nc.scalar.activation(own_sums[r][:].rearrange("k t (a p) -> k a t p", p=4),
+                                 banks[5 + r][:].rearrange("k (a p t) -> k a t p", p=4, t=4), COPY, scale=own_gate[:, r : r + 1])
+        sort(sums[:, 0:2], 0, 2, 2, 2)
+        finish(0, 3, [part[:] for part in own_sums])
+        finish(1, 1, [sums[:, 0]])
+        finish(2, 2, [sums[:, 1]])
+        for b in (2, 3):
+            combine(ring, (b - 2) * 2 * P, b, 3, [quarter(0, b - 2), quarter(0, b)])
+        sort(sums[:, 2:4], 0, 2, 2, 2)
+        finish(3, 5, [sums[:, 2]])
+        finish(4, 6, [sums[:, 3]])
+        for b in (2, 3):
+            combine(first, (b - 2) * 2 * P, b, 5, [quarter(0, b - 2)])
+        sort(last_sums[:], 0, 1, 2, 2)
+        finish(5, 7, [last_sums[:, 0]])
 
-        last = T // P - 1
-        cols = slice(last * P, T)
-        half_bank = [late_banks[0], back_banks[4]]
-        pairs = sb("pairs", [P, 2, P, 2], BF16)
-        plain = sb("plain", [P, 4 * P], F32)
-        for half in range(2):
-            for b in (2 * half, 2 * half + 1):
-                combine(first if half else ring, (b % 2) * 2 * P, b, last, 1, [half_bank[half][:, (b % 2) * P : (b % 2 + 1) * P]])
-            src = half_bank[half][:, 0 : 2 * P]
-            nc.scalar.copy(pairs[:, :, half * 64 : half * 64 + 64, :], src.rearrange("k (p u e) -> k u p e", u=2, e=2))
-            nc.scalar.copy(plain[:, half * 2 * P : (half + 1) * 2 * P], src)
-        pair_words = pairs[:].rearrange("k u p e -> k (u p e)").bitcast(F32)
-        for u in range(2):
-            nc.tensor.transpose(ybanks[2][:, u * P : (u + 1) * P], pair_words[:, u * P : (u + 1) * P], ident[:])
-        last_result = sb("last_result", [P, 4, P], F32)
-        for half in range(2):
-            bank = banks[5 + half]
-            for j in range(2):
-                b = 2 * half + j
-                nc.tensor.transpose(bank[:, j * P : (j + 1) * P], plain[:, b * P : (b + 1) * P], ident[:])
-            part = last_result[:, 2 * half : 2 * half + 2, :]
-            nc.scalar.copy(part, bank[:, 0 : 2 * P].rearrange("p (b k) -> p b k", b=2))
-            nc.sync.dma_start(out_blocks[:, 2 * half : 2 * half + 2, cols], part)
-
-        out_codes = sb("out_codes", [P, T], I32, tag="warm_in")
+        out_codes = sb("out_codes", [P, T], I32)
         out_scales = sb("out_scales", [P, T], U8)
-
-        rounded.append(sb("rounded1", [P, 2 * P, 4], BF16, tag="y3"))
-        rounded.append(sb("rounded2", [P, P, 4], BF16))
-
-        def quantise_out(g, at, t0, n):
-            nc.vector.quantize_mx(out_codes[:, t0 : t0 + n].bitcast(FP8X4), out_scales[:, t0 : t0 + n],
-                                  rounded[g][:, at : at + n, :].rearrange("p k t -> p (k t)"))
-
-        quantise_out(0, 0, 0, 2 * P)
-        nc.sync.dma_start(out_words[:, 0 : 2 * P], out_codes[:, 0 : 2 * P])
-        for c in (3, 4):
-            nc.vector.tensor_copy(rounded[1][:, (c - 3) * P : (c - 2) * P, :].rearrange("p (a k) t -> p a t k", k=4),
-                                  results[c][:].rearrange("p t (a k) -> p a t k", k=4))
-        quantise_out(0, 2 * P, 2 * P, P)
-        quantise_out(1, 0, 3 * P, 2 * P)
-        nc.sync.dma_start(out_words[:, 2 * P : last * P], out_codes[:, 2 * P : last * P])
-        nc.vector.tensor_copy(rounded[2][:].rearrange("p k t -> p (k t)").bitcast(F32).rearrange("p (k u) -> p k u", u=2),
-                              ybanks[2][:, 0 : 2 * P].rearrange("p (u k) -> p k u", u=2))
-        quantise_out(2, 0, last * P, P)
-        nc.scalar.dma_start(out_words[:, cols], out_codes[:, cols])
+        for g, (c0, n) in enumerate(((0, 3), (3, 2), (5, 1))):
+            rounded = sb("rounded%d" % g, [P, n * P, 4], BF16)
+            for j in range(n):
+                nc.vector.tensor_copy(rounded[:, j * P : (j + 1) * P, :].rearrange("p (a k) t -> p a t k", k=4),
+                                      results[c0 + j][:].rearrange("p t (a k) -> p a t k", k=4))
+            cols = slice(c0 * P, (c0 + n) * P)
+            nc.vector.quantize_mx(out_codes[:, cols].bitcast(FP8X4), out_scales[:, cols], rounded[:].rearrange("p k t -> p (k t)"))
+            (nc.scalar if g == 2 else nc.sync).dma_start(out_words[:, cols], out_codes[:, cols])
         for r in range(4):
             queue = nc.sync if r % 2 == 0 else nc.scalar
             queue.dma_start(out_2[0, r:16:4, :].bitcast(I32), out_scales[r:P:32, :].bitcast(I32))

@@ -209,8 +209,8 @@ def tile_moe_hot_mlp_silu_kernel(
 
         y = [sb("y%d" % b, [P, S], F32) for b in range(4)]
         y_banks = ((6, 3, 4, 2, 0), (4, 2, 0, 1, 4), (2, 0, 1, 4, 2), (0, 4, 2, 0, 4))
-        for u in range(20):
-            b, pair = divmod(u, 5)
+
+        def second_layer(b, pair):
             bank = banks[y_banks[b][pair]]
             at = max(b - 1, 0) * P
             experts = UNITS[pair]
@@ -224,7 +224,7 @@ def tile_moe_hot_mlp_silu_kernel(
                                     rhs_scale=h_scales[pair][:, half], start=True, stop=True)
             width = len(experts) * C
             dst = y[b][:, experts[0] * C : experts[0] * C + width]
-            if u in Y_ON_VECTOR:
+            if b == 0 and pair in Y_ON_VECTOR:
                 nc.vector.tensor_copy(dst, bank[:, 0:width])
             else:
                 nc.scalar.copy(dst, bank[:, 0:width])
@@ -267,27 +267,43 @@ def tile_moe_hot_mlp_silu_kernel(
             nc.scalar.copy(results[c][:], banks[bank][:].rearrange("p (t k) -> p t k", t=4))
             nc.sync.dma_start(out_rows[:, :, c * P : (c + 1) * P], results[c][:])
 
-        combine(first, 0, 0, 1, [quarter(1, j) for j in range(4)] + [quarter(4, 0)])
-        combine(ring, 0, 1, 1, [quarter(2, j) for j in range(4)] + [quarter(4, 1)])
-        for b in range(4):
+        def own_gathers(b):
             for r in range(TOP):
                 nc.scalar.activation(own[r][:, b * P : (b + 1) * P], y[b][:].indirect(pos_sb[r][:, 0 : P // 16]), COPY)
                 nc.tensor.transpose(quarter(5 + r, b), own[r][:, b * P : (b + 1) * P], ident[:])
+
+        def block(b):
+            for pair in range(len(UNITS)):
+                second_layer(b, pair)
+
+        def own_scaled():
+            for r in range(TOP):
+                nc.scalar.activation(own_sums[r][:].rearrange("k t (a p) -> k a t p", p=4),
+                                     banks[5 + r][:].rearrange("k (a p t) -> k a t p", p=4, t=4), COPY, scale=own_gate[:, r : r + 1])
+
+        block(0)
+        block(1)
+        own_gathers(0)
+        own_gathers(1)
+        block(2)
+        block(3)
+        combine(first, 0, 0, 1, [quarter(1, j) for j in range(4)] + [quarter(4, 0)])
+        combine(ring, 0, 1, 1, [quarter(2, j) for j in range(4)] + [quarter(4, 1)])
+        own_gathers(2)
+        own_gathers(3)
         for b in (2, 3):
             combine(first, (b - 2) * 2 * P, b, 1, [quarter(0, b - 2), quarter(0, b)])
         sort(sums[:], 1, 4, 0, 1)
         sort(sums[:], 2, 4, 1, 1)
         sort(last_sums[:], 4, 1, 0, 2)
-        for r in range(TOP):
-            nc.scalar.activation(own_sums[r][:].rearrange("k t (a p) -> k a t p", p=4),
-                                 banks[5 + r][:].rearrange("k (a p t) -> k a t p", p=4, t=4), COPY, scale=own_gate[:, r : r + 1])
         sort(sums[:, 0:2], 0, 2, 2, 2)
-        finish(0, 3, [part[:] for part in own_sums])
+        own_scaled()
         finish(1, 1, [sums[:, 0]])
         finish(2, 2, [sums[:, 1]])
         for b in (2, 3):
             combine(ring, (b - 2) * 2 * P, b, 3, [quarter(0, b - 2), quarter(0, b)])
         sort(sums[:, 2:4], 0, 2, 2, 2)
+        finish(0, 3, [part[:] for part in own_sums])
         finish(3, 5, [sums[:, 2]])
         finish(4, 6, [sums[:, 3]])
         for b in (2, 3):

@@ -254,8 +254,8 @@ def tile_moe_hot_mlp_silu_kernel(
         def quarter(bank, j):
             return banks[bank][:, j * P : (j + 1) * P]
 
-        def sort(dst, bank, chunks, b0, blocks):
-            nc.scalar.copy(dst[:, :, :, 32 * b0 : 32 * (b0 + blocks)].rearrange("k c t (a p) -> k c a t p", p=4),
+        def sort(dst, bank, chunks, b0, blocks, copy=nc.scalar.copy):
+            copy(dst[:, :, :, 32 * b0 : 32 * (b0 + blocks)].rearrange("k c t (a p) -> k c a t p", p=4),
                            banks[bank][:, 0 : chunks * blocks * P].rearrange("k (c a p t) -> k c a t p", c=chunks, p=4, t=4))
 
         def finish(c, bank, parts):
@@ -304,11 +304,11 @@ def tile_moe_hot_mlp_silu_kernel(
             combine(ring, (b - 2) * 2 * P, b, 3, [quarter(0, b - 2), quarter(0, b)])
         sort(sums[:, 2:4], 0, 2, 2, 2)
         finish(0, 3, [part[:] for part in own_sums])
+        for b in (2, 3):
+            combine(first, (b - 2) * 2 * P, b, 5, [quarter(2, b - 2)])
+        sort(last_sums[:], 2, 1, 2, 2)
         finish(3, 5, [sums[:, 2]])
         finish(4, 6, [sums[:, 3]])
-        for b in (2, 3):
-            combine(first, (b - 2) * 2 * P, b, 5, [quarter(0, b - 2)])
-        sort(last_sums[:], 0, 1, 2, 2)
         finish(5, 7, [last_sums[:, 0]])
 
         out_codes = sb("out_codes", [P, T], I32)
@@ -316,8 +316,11 @@ def tile_moe_hot_mlp_silu_kernel(
         for g, (c0, n) in enumerate(((0, 3), (3, 2), (5, 1))):
             rounded = sb("rounded%d" % g, [P, n * P, 4], BF16)
             for j in range(n):
-                nc.vector.tensor_copy(rounded[:, j * P : (j + 1) * P, :].rearrange("p (a k) t -> p a t k", k=4),
-                                      results[c0 + j][:].rearrange("p t (a k) -> p a t k", k=4))
+                if g == 2:
+                    nc.scalar.copy(rounded[:], banks[7][:].rearrange("p (t k) -> p k t", t=4))
+                else:
+                    nc.vector.tensor_copy(rounded[:, j * P : (j + 1) * P, :].rearrange("p (a k) t -> p a t k", k=4),
+                                          results[c0 + j][:].rearrange("p t (a k) -> p a t k", k=4))
             cols = slice(c0 * P, (c0 + n) * P)
             nc.vector.quantize_mx(out_codes[:, cols].bitcast(FP8X4), out_scales[:, cols], rounded[:].rearrange("p k t -> p (k t)"))
             (nc.scalar if g == 2 else nc.sync).dma_start(out_words[:, cols], out_codes[:, cols])

@@ -59,13 +59,9 @@ def tile_moe_hot_mlp_silu_kernel(
         s1c = sb("s1c", [P, COLD, H], U8)
         s2c = sb("s2c", [P, COLD, N], U8)
         ident = sb("ident", [P, P], F32)
-        warm_in = sb("warm_in", [P, 1], F32)
-        warm_out = sb("warm_out", [P, 1], F32)
 
         nc.vector.memset(s1c[:].bitcast(I32), 0)
         nc.vector.memset(s1h[:].bitcast(I32), 0)
-        nc.vector.memset(warm_in[:], 0.0)
-        nc.scalar.activation(warm_out[:], warm_in[:], SILU)
         nc.vector.memset(s2h[:].bitcast(I32), 0)
         nc.vector.memset(s2c[:].bitcast(I32), 0)
         make_identity(nc, ident[:])
@@ -124,7 +120,7 @@ def tile_moe_hot_mlp_silu_kernel(
         w2c.append(sb("w2c_rest", [P, COLD, (N - P) // 2], I32))
         nc.sync.dma_start(w2h[1][:], w2h_words_i[:, :, P:N])
         nc.sync.dma_start(w2c[1][:], w2c_words_i[:, :, P // 2 : N // 2])
-        gate_sb = sb("gate_sb", [P, TOP, T - P], F32, tag="warm_in")
+        gate_sb = sb("gate_sb", [P, TOP, T - P], F32)
         nc.sync.dma_start(gate_sb[:], gate[:, :, P:T].rearrange("r p t -> p r t"))
         for r, pos in enumerate((pos1, pos2, pos3)):
             nc.sync.dma_start(pos_sb[r][:], pos)

@@ -108,25 +108,19 @@ def tile_moe_hot_mlp_silu_kernel(
         for c in range(1, COLD - TURNED):
             deal_cold(c)
 
-        w2h_words_i = hot_words(w2h_words, 0, HOT)
-        w2c_words_i = w2c_words[:, 0].rearrange("e p b -> p e b").bitcast(I32)
-        w2h = [sb("w2h_first", [P, HOT, P], I32)]
-        w2c = [sb("w2c_first", [P, COLD, P // 2], I32)]
-        load_hot_scales(s2h, w2h_scales)
-        nc.sync.dma_start(w2h[0][:], w2h_words_i[:, :, 0:P])
-        nc.sync.dma_start(w2c[0][:], w2c_words_i[:, :, 0 : P // 2])
-        load_cold_scales(s2c, w2c_scales)
-        w2h.append(sb("w2h_rest", [P, HOT, N - P], I32))
-        w2c.append(sb("w2c_rest", [P, COLD, (N - P) // 2], I32))
-        nc.sync.dma_start(w2h[1][:], w2h_words_i[:, :, P:N])
-        nc.sync.dma_start(w2c[1][:], w2c_words_i[:, :, P // 2 : N // 2])
+        w2h = sb("w2h", [P, HOT, N], I32)
+        w2c = sb("w2c", [P, COLD, N // 2], I32)
         gate_sb = sb("gate_sb", [P, TOP, T - P], F32)
-        nc.sync.dma_start(gate_sb[:], gate[:, :, P:T].rearrange("r p t -> p r t"))
+        own_gate = sb("own_gate", [P, TOP], F32)
+        load_hot_scales(s2h, w2h_scales)
+        nc.sync.dma_start(w2h[:], hot_words(w2h_words, 0, HOT))
+        load_cold_scales(s2c, w2c_scales)
+        nc.sync.dma_start(w2c[:], w2c_words[:, 0].rearrange("e p b -> p e b").bitcast(I32))
         for r, pos in enumerate((pos1, pos2, pos3)):
             nc.sync.dma_start(pos_sb[r][:], pos)
-        own_gate = sb("own_gate", [P, TOP], F32)
         with nc.allow_non_contiguous_dma(reason="one weight a partition"):
             nc.sync.dma_start(own_gate[:], gate[:, 0, 0:P].rearrange("r p -> p r"))
+        nc.sync.dma_start(gate_sb[:], gate[:, :, P:T].rearrange("r p t -> p r t"))
 
         h_in = [sb("h_in%d" % j, [P, 4 * C * len(unit)], BF16) for j, unit in enumerate(UNITS)]
         h_scales = [sb("h_scales%d" % j, [P, C * len(unit)], U8) for j, unit in enumerate(UNITS)]
@@ -208,13 +202,13 @@ def tile_moe_hot_mlp_silu_kernel(
 
         def second_layer(b, pair):
             bank = banks[y_banks[b][pair]]
-            at = max(b - 1, 0) * P
+            at = b * P
             experts = UNITS[pair]
             for j, e in enumerate(experts):
                 if e < HOT:
-                    w, ws = w2h[min(b, 1)][:, e, at : at + P].bitcast(FP8X4), s2h[4 * e : P, b * P : (b + 1) * P]
+                    w, ws = w2h[:, e, at : at + P].bitcast(FP8X4), s2h[4 * e : P, b * P : (b + 1) * P]
                 else:
-                    w, ws = w2c[min(b, 1)][:, e - HOT, at // 2 : (at + P) // 2].bitcast(U8).bitcast(FP4X4), s2c[:, e - HOT, b * P : (b + 1) * P]
+                    w, ws = w2c[:, e - HOT, at // 2 : (at + P) // 2].bitcast(U8).bitcast(FP4X4), s2c[:, e - HOT, b * P : (b + 1) * P]
                 half = slice(j * C, (j + 1) * C)
                 nc.tensor.matmul_mx(bank[:, half], lhsT=w, lhsT_scale=ws, rhs=h_codes[pair][:, half].bitcast(FP8X4),
                                     rhs_scale=h_scales[pair][:, half], start=True, stop=True)

@@ -22,7 +22,7 @@ SILU = mybir.ActivationFunctionType.Silu
 COPY = mybir.ActivationFunctionType.Copy
 MULT = mybir.AluOpType.mult
 
-WORD_PIECES = [(128, None), (128, None), (256, None), (512, None), (512, "gs0"), (512, "gs1"), (256, "gw3")]
+WORD_PIECES = [(128, None), (128, None), (256, None), (256, None), (256, None), (256, "gs0"), (256, "gs1"), (256, "h_rows0"), (256, "h_rows1"), (256, "gw3")]
 BYTE_PIECES = [(256, None), (256, None), (512, "gw0"), (512, "gw1"), (512, "gw2"), (256, "w1c_a")]
 ORDER = (4, 5, 0, 1, 2, 3, 6, 7, 8)
 TURNED = 1
@@ -190,10 +190,7 @@ def tile_moe_hot_mlp_silu_kernel(
             first_layer(k, chunk_words[k], chunk_scales[k])
             if k % 2 == 1 and k < 2 * TURNED:
                 turn_and_weave(k // 2)
-            if k == 13:
-                quantise(0)
-                quantise(2, "w1c_dealt1")
-        for j in (1, 3, 4):
+        for j in (2, 0, 1, 3, 4):
             quantise(j)
 
 

@@ -51,7 +51,8 @@ def tile_moe_hot_mlp_silu_kernel(
         w1h = [sb("w1h_%d" % j, [P, n, H], I32) for j, n in enumerate((1, 1, 2))]
         w1c_a = sb("w1c_a", [P, 2, 2 * H], U8)
         w1c_b = sb("w1c_b", [P, 3, 2 * H], U8)
-        w1_dealt = [sb("w1_dealt%d" % e, [P, H], I32) for e in range(HOT)]
+        hot_dealt = [sb("w1_dealt%d" % j, [P, n, H], I32) for j, n in enumerate((1, 1, 2))]
+        w1_dealt = [hot_dealt[min(e, 2)][:, max(e - 2, 0), :] for e in range(HOT)]
         w1c_dealt = [sb("w1c_dealt%d" % c, [P, 2 * H], U8) for c in range(COLD - TURNED)]
         s1_dealt = sb("s1_dealt", [P, H], U8)
         s1h = sb("s1h", [P, H], U8)
@@ -91,22 +92,20 @@ def tile_moe_hot_mlp_silu_kernel(
         nc.sync.dma_start(w1c_b[:].bitcast(I32), w1c_words[2:COLD, 0].rearrange("e p b -> p e b").bitcast(I32))
 
         def deal(dst, src, run):
-            nc.gpsimd.tensor_copy(dst.rearrange("p (t a i) -> p a t i", t=4, i=run), src.rearrange("p (a i t) -> p a t i", t=4, i=run))
+            nc.gpsimd.tensor_copy(dst.rearrange("p e (t a i) -> p e a t i", t=4, i=run),
+                                  src.rearrange("p e (a i t) -> p e a t i", t=4, i=run))
 
-        def deal_cold(c):
-            deal(s1c_dealt[c], s1c[:, TURNED + c, :], 16)
-            words = w1c_b[:, c - 1, :] if c else w1c_a[:, 1, :]
-            deal(w1c_dealt[c][:].bitcast(U16), words.bitcast(U16), 8)
-
-        early_plane = sb("early_plane", [P, H], U8)
+        early_plane = sb("early_plane", [P, 1, H], U8)
         late_planes = sb("late_planes", [P, 3, H], U8, tag="w1h_2")
-        s1c_dealt = [early_plane[:]] + [late_planes[:, j, :] for j in range(3)]
-        deal_cold(0)
-        deal(s1_dealt[:], s1h[:], 16)
-        for e in range(HOT):
-            deal(w1_dealt[e][:], w1h[min(e, 2)][:, max(e - 2, 0), :], 4)
+        s1c_dealt = [early_plane[:, 0, :]] + [late_planes[:, j, :] for j in range(3)]
+        deal(early_plane[:], s1c[:, 1:2, :], 16)
+        deal(w1c_dealt[0][:].bitcast(U16).unsqueeze(1), w1c_a[:, 1:2, :].bitcast(U16), 8)
+        deal(s1_dealt[:].unsqueeze(1), s1h[:].unsqueeze(1), 16)
+        for j, tile in enumerate(hot_dealt):
+            deal(tile[:], w1h[j][:], 4)
+        deal(late_planes[:], s1c[:, 2:COLD, :], 16)
         for c in range(1, COLD - TURNED):
-            deal_cold(c)
+            deal(w1c_dealt[c][:].bitcast(U16).unsqueeze(1), w1c_b[:, c - 1 : c, :].bitcast(U16), 8)
 
         w2h = sb("w2h", [P, HOT, N], I32)
         w2c = sb("w2c", [P, COLD, N // 2], I32)

@@ -103,8 +103,10 @@ def tile_moe_hot_mlp_silu_kernel(
         deal(s1_dealt[:].unsqueeze(1), s1h[:].unsqueeze(1), 16)
         for j, tile in enumerate(hot_dealt):
             deal(tile[:], w1h[j][:], 4)
-        deal(late_planes[:], s1c[:, 2:COLD, :], 16)
+        deal(late_planes[:, 0:2, :], s1c[:, 2:4, :], 16)
         for c in range(1, COLD - TURNED):
+            if c == 3:
+                deal(late_planes[:, 2:3, :], s1c[:, 4:5, :], 16)
             deal(w1c_dealt[c][:].bitcast(U16).unsqueeze(1), w1c_b[:, c - 1 : c, :].bitcast(U16), 8)
 
         w2h = sb("w2h", [P, HOT, N], I32)
@@ -152,8 +154,8 @@ def tile_moe_hot_mlp_silu_kernel(
                     nc.tensor.matmul_mx(bank[:, cols], lhsT=w, lhsT_scale=ws,
                                         rhs=words.bitcast(FP8X4), rhs_scale=scales, start=True, stop=True)
                 at = (k % 2) * 4 * P
-                nc.scalar.activation(h_place(e)[:, at : at + 4 * P].rearrange("p (s t) -> p s t", t=4),
-                                     bank[:].rearrange("p (t s) -> p s t", t=4), SILU)
+                nc.scalar.activation(h_place(e)[:, at : at + 4 * P].rearrange("p (a i t) -> p a t i", t=4, i=2),
+                                     bank[:].rearrange("p (t a i) -> p a t i", t=4, i=2), SILU)
                 return
             c = e - HOT
             w, ws = (w1c_a[:, c, :] if c < 2 else w1c_b[:, c - 2, :]).bitcast(FP4X4), s1c[:, c, :]
@@ -299,17 +301,34 @@ def tile_moe_hot_mlp_silu_kernel(
 
         out_codes = sb("out_codes", [P, T], I32)
         out_scales = sb("out_scales", [P, T], U8)
-        for g, (c0, n) in enumerate(((0, 3), (3, 2), (5, 1))):
-            rounded = sb("rounded%d" % g, [P, n * P, 4], BF16)
-            for j in range(n):
-                if g == 2:
-                    nc.scalar.copy(rounded[:], banks[7][:].rearrange("p (t k) -> p k t", t=4))
-                else:
-                    nc.vector.tensor_copy(rounded[:, j * P : (j + 1) * P, :].rearrange("p (a k) t -> p a t k", k=4),
-                                          results[c0 + j][:].rearrange("p t (a k) -> p a t k", k=4))
+        rounded = [sb("rounded%d" % g, [P, 2 * P, 4], BF16) for g in range(3)]
+
+        def round_chunk(c):
+            nc.vector.tensor_copy(rounded[c // 2][:, c % 2 * P : (c % 2 + 1) * P, :].rearrange("p (a k) t -> p a t k", k=4),
+                                  results[c][:].rearrange("p t (a k) -> p a t k", k=4))
+
+        def quantise_out(c0, n):
             cols = slice(c0 * P, (c0 + n) * P)
-            nc.vector.quantize_mx(out_codes[:, cols].bitcast(FP8X4), out_scales[:, cols], rounded[:].rearrange("p k t -> p (k t)"))
-            (nc.scalar if g == 2 else nc.sync).dma_start(out_words[:, cols], out_codes[:, cols])
+            nc.vector.quantize_mx(out_codes[:, cols].bitcast(FP8X4), out_scales[:, cols],
+                                  rounded[c0 // 2][:, c0 % 2 * P : (c0 % 2 + n) * P, :].rearrange("p k t -> p (k t)"))
+
+        def store_words(c0, n, queue):
+            cols = slice(c0 * P, (c0 + n) * P)
+            queue.dma_start(out_words[:, cols], out_codes[:, cols])
+
+        for c in (1, 0, 2):
+            round_chunk(c)
+        quantise_out(0, 2)
+        store_words(0, 2, nc.sync)
+        round_chunk(3)
+        round_chunk(4)
+        quantise_out(2, 2)
+        quantise_out(4, 1)
+        store_words(2, 3, nc.sync)
+        nc.scalar.copy(rounded[2][:, P : 2 * P, :].rearrange("p (a i) t -> p a t i", i=2),
+                       banks[7][:].rearrange("p (t a i) -> p a t i", t=4, i=2))
+        quantise_out(5, 1)
+        store_words(5, 1, nc.scalar)
         for r in range(4):
             queue = nc.sync if r % 2 == 0 else nc.scalar
             queue.dma_start(out_2[0, r:16:4, :].bitcast(I32), out_scales[r:P:32, :].bitcast(I32))

from contextlib import ExitStack

import concourse.mybir as mybir
from concourse.masks import make_identity

K, T, E, C, H, N, HOT = 512, 768, 9, 256, 512, 512, 4
COLD = E - HOT
TOP = 3
S = E * C
P = 128
FLOPS = 2 * S * (K * H + H * N)

F32 = mybir.dt.float32
BF16 = mybir.dt.bfloat16
I32 = mybir.dt.int32
U32 = mybir.dt.uint32
U16 = mybir.dt.uint16
U8 = mybir.dt.uint8
FP8X4 = mybir.dt.float8_e4m3fn_x4
FP4X4 = mybir.dt.float4_e2m1fn_x4
SILU = mybir.ActivationFunctionType.Silu
COPY = mybir.ActivationFunctionType.Copy
MULT = mybir.AluOpType.mult

WORD_PIECES = [(128, None), (128, None), (256, None), (256, None), (256, None), (256, "gs0"), (256, "gs1"), (256, "h_rows0"), (256, "h_rows1"), (256, "gw3")]
BYTE_PIECES = [(256, None), (256, None), (512, "gw0"), (512, "gw1"), (512, "gw2"), (256, "w1c_a")]
ORDER = (4, 5, 0, 1, 2, 3, 6, 7, 8)
TURNED = 1
UNITS = ((0, 1), (2, 3), (4, 5), (6, 7), (8,))
Y_ON_VECTOR = (0, 3)


def tile_moe_hot_mlp_silu_kernel(
    tc, x_words, x_scales, w1h_words, w1h_scales, w2h_words, w2h_scales, w1c_words, w1c_scales,
    w2c_words, w2c_scales, gate, offs, pos1, pos2, pos3, out_0, out_1, out_2,
):
    nc = tc.nc
    with ExitStack() as ctx:
        keep = ctx.enter_context(tc.tile_pool(name="keep", bufs=1))
        psum = ctx.enter_context(tc.psum_pool(name="psum", bufs=1))

        def sb(name, shape, dtype, tag=None):
            return keep.tile(shape, dtype, name=name, tag=tag or name, align_bytes=64)

        banks = [psum.tile([P, 512], F32, name="bank%d" % b) for b in range(8)]

        offs_sb = sb("offs_sb", [P, S // 16], U16)
        pos_sb = [sb("pos_sb%d" % r, [P, T // 16], U16) for r in range(TOP)]
        xw = sb("xw", [P, T], I32)
        xs = sb("xs", [P, T], U8)
        w1h = [sb("w1h_%d" % j, [P, n, H], I32) for j, n in enumerate((1, 1, 2))]
        w1c_a = sb("w1c_a", [P, 2, 2 * H], U8)
        w1c_b = sb("w1c_b", [P, 3, 2 * H], U8)
        hot_dealt = [sb("w1_dealt%d" % j, [P, n, H], I32) for j, n in enumerate((1, 1, 2))]
        w1_dealt = [hot_dealt[min(e, 2)][:, max(e - 2, 0), :] for e in range(HOT)]
        w1c_dealt = [sb("w1c_dealt%d" % c, [P, 2 * H], U8) for c in range(COLD - TURNED)]
        s1_dealt = sb("s1_dealt", [P, H], U8)
        s1h = sb("s1h", [P, H], U8)
        s2h = sb("s2h", [P, N], U8)
        s1c = sb("s1c", [P, COLD, H], U8)
        s2c = sb("s2c", [P, COLD, N], U8)
        ident = sb("ident", [P, P], F32)

        nc.vector.memset(s1c[:].bitcast(I32), 0)
        nc.vector.memset(s1h[:].bitcast(I32), 0)
        nc.vector.memset(s2h[:].bitcast(I32), 0)
        nc.vector.memset(s2c[:].bitcast(I32), 0)
        make_identity(nc, ident[:])

        def load_hot_scales(dst, src):
            for q in range(4):
                nc.sync.dma_start(dst[32 * q : 32 * q + 16, :].bitcast(I32), src[:, 0, 4 * q : 4 * q + 4, :].bitcast(I32))

        def load_cold_scales(dst, src):
            for r in range(4):
                nc.sync.dma_start(dst[r:P:32].bitcast(I32), src[:, 0, r:16:4, :].rearrange("e q c -> q e c").bitcast(I32))

        def hot_words(src, lo, hi):
            return src[lo:hi, 0].rearrange("e p c d -> p e (c d)").bitcast(I32)

        for r in range(4):
            nc.sync.dma_start(xs[32 * r : 32 * r + 32, :].bitcast(I32),
                              x_scales[0, 4 * r : 4 * r + 4, :].bitcast(I32).unsqueeze(0).to_broadcast([8, 4, T // 4]))
        nc.sync.dma_start(offs_sb[:], offs)
        nc.sync.dma_start(xw[:], x_words[0].rearrange("p t d -> p (t d)").bitcast(I32))
        nc.sync.dma_start(w1c_a[:].bitcast(I32), w1c_words[0:2, 0].rearrange("e p b -> p e b").bitcast(I32))
        load_cold_scales(s1c, w1c_scales)
        nc.sync.dma_start(w1h[0][:], hot_words(w1h_words, 0, 1))
        load_hot_scales(s1h, w1h_scales)
        nc.sync.dma_start(w1h[1][:], hot_words(w1h_words, 1, 2))
        nc.sync.dma_start(w1h[2][:], hot_words(w1h_words, 2, HOT))
        nc.sync.dma_start(w1c_b[:].bitcast(I32), w1c_words[2:COLD, 0].rearrange("e p b -> p e b").bitcast(I32))

        def deal(dst, src, run):
            nc.gpsimd.tensor_copy(dst.rearrange("p e (t a i) -> p e a t i", t=4, i=run),
                                  src.rearrange("p e (a i t) -> p e a t i", t=4, i=run))

        early_plane = sb("early_plane", [P, 1, H], U8)
        late_planes = sb("late_planes", [P, 3, H], U8, tag="w1h_2")
        s1c_dealt = [early_plane[:, 0, :]] + [late_planes[:, j, :] for j in range(3)]
        deal(early_plane[:], s1c[:, 1:2, :], 16)
        deal(w1c_dealt[0][:].bitcast(U16).unsqueeze(1), w1c_a[:, 1:2, :].bitcast(U16), 8)
        deal(s1_dealt[:].unsqueeze(1), s1h[:].unsqueeze(1), 16)
        for j, tile in enumerate(hot_dealt):
            deal(tile[:], w1h[j][:], 4)
        deal(late_planes[:, 0:2, :], s1c[:, 2:4, :], 16)
        for c in range(1, COLD - TURNED):
            if c == 3:
                deal(late_planes[:, 2:3, :], s1c[:, 4:5, :], 16)
            deal(w1c_dealt[c][:].bitcast(U16).unsqueeze(1), w1c_b[:, c - 1 : c, :].bitcast(U16), 8)

        w2h = sb("w2h", [P, HOT, N], I32)
        w2c = sb("w2c", [P, COLD, N // 2], I32)
        gate_sb = sb("gate_sb", [P, TOP, T - P], F32)
        own_gate = sb("own_gate", [P, TOP], F32)
        load_hot_scales(s2h, w2h_scales)
        nc.sync.dma_start(w2h[:], hot_words(w2h_words, 0, HOT))
        load_cold_scales(s2c, w2c_scales)
        nc.sync.dma_start(w2c[:], w2c_words[:, 0].rearrange("e p b -> p e b").bitcast(I32))
        for r, pos in enumerate((pos1, pos2, pos3)):
            nc.sync.dma_start(pos_sb[r][:], pos)
        with nc.allow_non_contiguous_dma(reason="one weight a partition"):
            nc.sync.dma_start(own_gate[:], gate[:, 0, 0:P].rearrange("r p -> p r"))
        nc.sync.dma_start(gate_sb[:], gate[:, :, P:T].rearrange("r p t -> p r t"))

        h_in = [sb("h_in%d" % j, [P, 4 * C * len(unit)], BF16) for j, unit in enumerate(UNITS)]
        h_scales = [sb("h_scales%d" % j, [P, C * len(unit)], U8) for j, unit in enumerate(UNITS)]
        h_rows = [sb("h_rows%d" % k, [P, H], BF16) for k in range(2 * TURNED)]
        h_codes = {}

        def h_place(e):
            j = [e in unit for unit in UNITS].index(True)
            at = UNITS[j].index(e) * 4 * C
            return h_in[j][:, at : at + 4 * C]

        def gather(name, window, dtype, pieces, j):
            done, (n, tag) = sum(piece[0] for piece in pieces[:j]), pieces[j]
            slot0 = ORDER[done // C] * C + done % C
            dst = sb("%s%d" % (name, j), [P, n], dtype, tag=tag)
            nc.vector.tensor_copy(dst[:], window.indirect(offs_sb[:, slot0 // 16 : (slot0 + n) // 16]))
            return [dst[:, c * P : (c + 1) * P] for c in range(n // P)]

        def first_layer(k, words, scales):
            e = ORDER[k // 2]
            bank = banks[k % 5]
            if k >= 2 * TURNED:
                for t in range(4):
                    cols = slice(t * P, (t + 1) * P)
                    if e < HOT:
                        w, ws = w1_dealt[e][:, cols].bitcast(FP8X4), s1_dealt[4 * e : P, cols]
                    else:
                        c = e - HOT - TURNED
                        w, ws = w1c_dealt[c][:, 2 * t * P : 2 * (t + 1) * P].bitcast(FP4X4), s1c_dealt[c][:, cols]
                    nc.tensor.matmul_mx(bank[:, cols], lhsT=w, lhsT_scale=ws,
                                        rhs=words.bitcast(FP8X4), rhs_scale=scales, start=True, stop=True)
                at = (k % 2) * 4 * P
                nc.scalar.activation(h_place(e)[:, at : at + 4 * P].rearrange("p (a i t) -> p a t i", t=4, i=2),
                                     bank[:].rearrange("p (t a i) -> p a t i", t=4, i=2), SILU)
                return
            c = e - HOT
            w, ws = (w1c_a[:, c, :] if c < 2 else w1c_b[:, c - 2, :]).bitcast(FP4X4), s1c[:, c, :]
            nc.tensor.matmul_mx(bank[:], lhsT=words.bitcast(FP8X4), lhsT_scale=scales,
                                rhs=w, rhs_scale=ws, start=True, stop=True)
            nc.scalar.activation(h_rows[k][:].rearrange("s (u p e) -> s u p e", u=2, e=2),
                                 bank[:].rearrange("s (p u e) -> s u p e", u=2, e=2), SILU)

        def turn_and_weave(e):
            bank = banks[5 + e]
            for c in range(2):
                words = h_rows[2 * e + c][:].bitcast(F32)
                for u in range(2):
                    col = (2 * c + u) * P
                    nc.tensor.transpose(bank[:, col : col + P], words[:, u * P : (u + 1) * P], ident[:])
            dst = h_place(HOT + e).bitcast(F32).rearrange("p (c s u) -> p c s u", c=2, u=2)
            src = bank[:].rearrange("p (c u s) -> p c s u", c=2, u=2)
            nc.vector.tensor_copy(dst, src)

        def quantise(j, tag=None):
            h_codes[j] = sb("h_codes%d" % j, [P, C * len(UNITS[j])], U32, tag=tag)
            nc.vector.quantize_mx(h_codes[j][:].bitcast(FP8X4), h_scales[j][:], h_in[j][:])

        chunk_words, chunk_scales = [], []
        word_piece = byte_piece = 0
        for k in range(S // P):
            if k == len(chunk_scales):
                chunk_scales.extend(gather("gs", xs[:], U8, BYTE_PIECES, byte_piece))
                byte_piece = byte_piece + 1
            if k == len(chunk_words):
                chunk_words.extend(gather("gw", xw[:].bitcast(U32), U32, WORD_PIECES, word_piece))
                word_piece = word_piece + 1
            first_layer(k, chunk_words[k], chunk_scales[k])
            if k % 2 == 1 and k < 2 * TURNED:
                turn_and_weave(k // 2)
        for j in (2, 0, 1, 3, 4):
            quantise(j)


        y = [sb("y%d" % b, [P, S], F32) for b in range(4)]
        y_banks = ((6, 3, 4, 2, 0), (4, 2, 0, 1, 4), (2, 0, 1, 4, 2), (0, 4, 2, 0, 4))

        def second_layer(b, pair):
            bank = banks[y_banks[b][pair]]
            at = b * P
            experts = UNITS[pair]
            for j, e in enumerate(experts):
                if e < HOT:
                    w, ws = w2h[:, e, at : at + P].bitcast(FP8X4), s2h[4 * e : P, b * P : (b + 1) * P]
                else:
                    w, ws = w2c[:, e - HOT, at // 2 : (at + P) // 2].bitcast(U8).bitcast(FP4X4), s2c[:, e - HOT, b * P : (b + 1) * P]
                half = slice(j * C, (j + 1) * C)
                nc.tensor.matmul_mx(bank[:, half], lhsT=w, lhsT_scale=ws, rhs=h_codes[pair][:, half].bitcast(FP8X4),
                                    rhs_scale=h_scales[pair][:, half], start=True, stop=True)
            width = len(experts) * C
            dst = y[b][:, experts[0] * C : experts[0] * C + width]
            if b == 0 and pair in Y_ON_VECTOR:
                nc.vector.tensor_copy(dst, bank[:, 0:width])
            else:
                nc.scalar.copy(dst, bank[:, 0:width])

        first = [sb("first%d" % r, [P, 5 * P], F32) for r in range(TOP)]
        ring = [sb("ring%d" % r, [P, 5 * P], F32) for r in range(TOP)]
        own = [sb("own%d" % r, [P, 4 * P], F32) for r in range(TOP)]
        own_sums = [sb("own_sums%d" % r, [P, 4, P], F32) for r in range(TOP)]
        sums = sb("sums", [P, 4, 4, P], F32)
        last_sums = sb("last_sums", [P, 1, 4, P], F32)
        out_rows = out_0.rearrange("(p t) k -> p t k", t=4)
        out_words = out_1[0].rearrange("p t d -> p (t d)").bitcast(I32)
        results = {}

        def combine(tiles, col, b, c0, targets):
            count = len(targets)
            for r in range(TOP):
                t0 = c0 * P
                nc.vector.tensor_tensor(tiles[r][:, col : col + count * P],
                                        y[b][:].indirect(pos_sb[r][:, t0 // 16 : (t0 + count * P) // 16]),
                                        gate_sb[:, r, t0 - P : t0 - P + count * P], MULT)
            for j in range(count):
                for r in range(TOP):
                    nc.tensor.matmul(targets[j], lhsT=tiles[r][:, col + j * P : col + (j + 1) * P], rhs=ident[:],
                                     is_transpose=True, start=(r == 0), stop=(r == TOP - 1))

        def quarter(bank, j):
            return banks[bank][:, j * P : (j + 1) * P]

        def sort(dst, bank, chunks, b0, blocks, copy=nc.scalar.copy):
            copy(dst[:, :, :, 32 * b0 : 32 * (b0 + blocks)].rearrange("k c t (a p) -> k c a t p", p=4),
                           banks[bank][:, 0 : chunks * blocks * P].rearrange("k (c a p t) -> k c a t p", c=chunks, p=4, t=4))

        def finish(c, bank, parts):
            for t in range(4):
                for j, part in enumerate(parts):
                    nc.tensor.matmul(quarter(bank, t), lhsT=part[:, t, :], rhs=ident[:],
                                     is_transpose=True, start=(j == 0), stop=(j == len(parts) - 1))
            results[c] = sb("result%d" % c, [P, 4, P], F32)
            nc.scalar.copy(results[c][:], banks[bank][:].rearrange("p (t k) -> p t k", t=4))
            nc.sync.dma_start(out_rows[:, :, c * P : (c + 1) * P], results[c][:])

        def own_gathers(b):
            for r in range(TOP):
                nc.scalar.activation(own[r][:, b * P : (b + 1) * P], y[b][:].indirect(pos_sb[r][:, 0 : P // 16]), COPY)
                nc.tensor.transpose(quarter(5 + r, b), own[r][:, b * P : (b + 1) * P], ident[:])

        def block(b):
            for pair in range(len(UNITS)):
                second_layer(b, pair)

        def own_scaled():
            for r in range(TOP):
                nc.scalar.activation(own_sums[r][:].rearrange("k t (a p) -> k a t p", p=4),
                                     banks[5 + r][:].rearrange("k (a p t) -> k a t p", p=4, t=4), COPY, scale=own_gate[:, r : r + 1])

        block(0)
        block(1)
        own_gathers(0)
        own_gathers(1)
        block(2)
        block(3)
        combine(first, 0, 0, 1, [quarter(1, j) for j in range(4)] + [quarter(4, 0)])
        combine(ring, 0, 1, 1, [quarter(2, j) for j in range(4)] + [quarter(4, 1)])
        own_gathers(2)
        own_gathers(3)
        for b in (2, 3):
            combine(first, (b - 2) * 2 * P, b, 1, [quarter(0, b - 2), quarter(0, b)])
        sort(sums[:], 1, 4, 0, 1)
        sort(sums[:], 2, 4, 1, 1)
        sort(last_sums[:], 4, 1, 0, 2)
        sort(sums[:, 0:2], 0, 2, 2, 2)
        own_scaled()
        finish(1, 1, [sums[:, 0]])
        finish(2, 2, [sums[:, 1]])
        for b in (2, 3):
            combine(ring, (b - 2) * 2 * P, b, 3, [quarter(0, b - 2), quarter(0, b)])
        sort(sums[:, 2:4], 0, 2, 2, 2)
        finish(0, 3, [part[:] for part in own_sums])
        for b in (2, 3):
            combine(first, (b - 2) * 2 * P, b, 5, [quarter(2, b - 2)])
        sort(last_sums[:], 2, 1, 2, 2)
        finish(3, 5, [sums[:, 2]])
        finish(4, 6, [sums[:, 3]])
        finish(5, 7, [last_sums[:, 0]])

        out_codes = sb("out_codes", [P, T], I32)
        out_scales = sb("out_scales", [P, T], U8)
        rounded = [sb("rounded%d" % g, [P, 2 * P, 4], BF16) for g in range(3)]

        def round_chunk(c):
            nc.vector.tensor_copy(rounded[c // 2][:, c % 2 * P : (c % 2 + 1) * P, :].rearrange("p (a k) t -> p a t k", k=4),
                                  results[c][:].rearrange("p t (a k) -> p a t k", k=4))

        def quantise_out(c0, n):
            cols = slice(c0 * P, (c0 + n) * P)
            nc.vector.quantize_mx(out_codes[:, cols].bitcast(FP8X4), out_scales[:, cols],
                                  rounded[c0 // 2][:, c0 % 2 * P : (c0 % 2 + n) * P, :].rearrange("p k t -> p (k t)"))

        def store_words(c0, n, queue):
            cols = slice(c0 * P, (c0 + n) * P)
            queue.dma_start(out_words[:, cols], out_codes[:, cols])

        for c in (1, 0, 2):
            round_chunk(c)
        quantise_out(0, 2)
        store_words(0, 2, nc.sync)
        round_chunk(3)
        round_chunk(4)
        quantise_out(2, 2)
        quantise_out(4, 1)
        store_words(2, 3, nc.sync)
        nc.scalar.copy(rounded[2][:, P : 2 * P, :].rearrange("p (a i) t -> p a t i", i=2),
                       banks[7][:].rearrange("p (t a i) -> p a t i", t=4, i=2))
        quantise_out(5, 1)
        store_words(5, 1, nc.scalar)
        for r in range(4):
            queue = nc.sync if r % 2 == 0 else nc.scalar
            queue.dma_start(out_2[0, r:16:4, :].bitcast(I32), out_scales[r:P:32, :].bitcast(I32))
